import numpy as np, ml_dtypes
CORES = [40,64,80,88,96,104,120,144]
N = 8
BF = ml_dtypes.bfloat16
C, T, S, DQ = 1024, 128, 3, 7
PL = N * C; FREE = 31
RANGES = (("mem", 0, 63), ("h", 0, 63), ("pnd", 0, PL - 1), ("due", 0, FREE), ("val", 0, 63), ("w", 0, 255), ("kap", 0, 255), ("th", 0, 1008))
def parts(rng):
    tops = rng.integers(24, 64, (1, 8, 16))
    nm = np.add.accumulate(rng.integers(1, PL // 16, (N, 8, T, 16)), axis=3) + rng.integers(0, PL, (N, 8, T, 1))
    nm = rng.permuted(nm & (PL - 1), axis=3)
    du = np.where(rng.random((N, 8, T, 16)) < 0.2, FREE, rng.integers(0, 9, (N, 8, T, 16))); du[..., :S] = FREE
    return {"mem": (rng.random((N, 8, 16, C)) * (tops[..., None] + 1)).astype(np.int64), "h": rng.integers(0, 64, (N, 8, 16, T)),
            "val": (rng.random((N, 8, 16, T, 16)) * (tops[..., None, None] + 1)).astype(np.int64), "nm": nm, "du": du,
            "w": rng.integers(0, 256, (N, 8, 16)), "kap": rng.integers(0, 256, (N, 8, 16)),
            "th": (np.sum(tops, axis=2) * (0.8 + 0.13 * rng.random((N, 8)))).astype(np.int64)}
def pack(p):
    bf = lambda a: np.ascontiguousarray(a).astype(np.float32).astype(BF)
    i4 = lambda a: np.ascontiguousarray(a).astype(np.int32)
    return {"mem": bf(p["mem"].reshape(N, 128, C)), "h": bf(p["h"].reshape(N, 128, T)),
            "pnd": i4(p["nm"].transpose(0, 1, 3, 2).reshape(N, 128, T)), "due": i4(p["du"].transpose(0, 1, 3, 2).reshape(N, 128, T)),
            "val": bf(p["val"].reshape(N, 128, 16 * T)), "w": i4(p["w"].reshape(N, 128, 1)), "kap": i4(p["kap"].reshape(N, 128, 1)),
            "th": i4(np.repeat(p["th"].reshape(N, 8, 1), 16, axis=2).reshape(N, 128, 1))}
def setup_inputs(rng):
    return pack(parts(rng))
def setup_inputs_corners(rng):
    p = parts(rng); s = np.arange(16); own = p["nm"]; mode = rng.integers(0, 7, (N, 8, T, 1)); mode[..., T - 1, 0] = 4; mode[..., 0, 0] = 1
    e = rng.integers(0, S + 1, (N, 8, T, 1)); q = rng.choice(np.array([0, 1, S - 1, S, 30]), (N, 8, T, 16))
    late = 30 - (rng.random((N, 8, T, 16)) * rng.integers(2, 16, (N, 8, T, 1))).astype(np.int64)
    border = C * rng.integers(0, N, (N, 8, T, 1)) - 8; border[..., T - 1, 0] = -8
    du = np.where(mode == 3, np.where(s == 15, 0, FREE), q); du = np.where(mode == 6, late, du)
    du = np.where(mode == 2, np.where(s == 15, e, 30), du); du = np.where(mode == 1, e, du); du = np.where(mode == 0, FREE, du)
    du[..., :S] = FREE
    nm = np.where(mode == 4, (border + s) & (PL - 1), own)
    nm = np.where(mode == 0, (PL - 1) * rng.integers(0, 2, (N, 8, T, 16)), nm)
    p["w"][:, 2] = 0; p["w"][:, 5] = 255; p["kap"][:, 3] = 0; p["kap"][:, 4] = 255; p["th"][:, 1] = 0; p["th"][:, 6] = 1008
    p["th"][1:3] = 1008
    z = slice(T - 8, T); nm[2, 2, z] = own[2, 2, z]; du[2, 2, z] = FREE; du[2, 2, z, 13] = 30; du[2, 2, z, 15] = 0
    p["val"][2, 2, :, z, 13] = 63; p["val"][2, 2, :, z, 15] = 0
    nm[1, 5] = own[1, 5]; du[1, 5, :, S:] = 30
    p["th"][0, 0] = 0; du[0, 0] = FREE
    for r in (0, N - 1):
        p["th"][r, 4] = 0; nm[r, 4] = own[0, 4]; du[r, 4] = FREE; du[r, 4, :, 15] = 0
    du[0, 4, :, 14] = 1
    p["nm"] = nm; p["du"] = du
    return pack(p)
def setup_inputs_crowd(rng):
    p = parts(rng); s = np.arange(16); i = np.arange(T).reshape(1, 1, T, 1); r = np.arange(N).reshape(N, 1, 1, 1)
    owner = rng.integers(0, N, (N, 8, 1, 1)); owner[:, 2] = 0; owner[:, 5] = N - 1; owner[N - 1] = 0
    col = np.broadcast_to(64 + i + 17 * s, (N, 8, T, 16)).copy(); far = (T * (r + 1) + i + 17 * s) % C
    col[:, 2] = far[:, 0]; col[:, 5] = far[:, 0]
    p["nm"] = C * owner + col
    du = np.zeros((N, 8, T, 16), np.int64); du[..., :S] = FREE; du[:, 2, :, 1::2] = FREE; du[N - 1, :, :, 1::2] = FREE; p["du"] = du
    p["w"][:, 2] = 0; p["w"][N - 1] = 0; p["th"][:] = 0
    return pack(p)
def edge(rng, a, b):
    k = rng.integers(0, 3, a)
    return 63 * np.where(k == 2, rng.integers(0, 2, b), k)
def setup_inputs_ends(rng):
    p = parts(rng); s = np.arange(16)
    mem = edge(rng, (N, 8, 1, C), (N, 8, 16, C)); mem[..., 0] = 0; mem[..., C - 1] = 63
    h = edge(rng, (N, 8, 1, T), (N, 8, 16, T)); val = edge(rng, (N, 8, 1, T, 16), (N, 8, 16, T, 16))
    for g in (1, 5, 7): mem[:, g, 3] = 0
    for g in (1, 5): val[:, g, 3] = 0
    w = 255 * rng.integers(0, 2, (N, 8, 16)); w[:, 1::2, 15] = 65; w[:, 6] = 255
    kap = 255 * rng.integers(0, 2, (N, 8, 16)); kap[:, 1::2, 15] = 255; kap[:, 1::2, 0] = 0
    th = 1008 * rng.integers(0, 2, (N, 8)); th[:, 0] = 0; th[:, 4] = 1008; th[:, 1::2] = 1008; th[0::2, 6] = 1008
    h[:, 1::2, :, T - 1] = 0; h[:, 1::2, 15, T - 1] = 63
    h[:, 6, :, T - 1] = 63; h[:, 0::4, :, T - 1] = 0
    few = rng.random((N, 8, T, 1)) < 0.7
    s1 = rng.integers(S, 16, (N, 8, T, 1)); s2 = S + (s1 - S + rng.integers(1, 16 - S, (N, 8, T, 1))) % (16 - S)
    nm = np.where(s == s1, 0, np.where(s == s2, PL - 1, (PL - 1) * rng.integers(0, 2, (N, 8, T, 16))))
    du = np.where(((s == s1) | (s == s2)) & (rng.random((N, 8, T, 16)) < 0.75), 0, FREE)
    nm = np.where(few, nm, p["nm"]); du = np.where(few, du, np.where((s >= S) & (rng.random((N, 8, T, 16)) < 0.6), 0, FREE))
    nm[:, 0::4, T - 1] = 0; du[:, 0::4, T - 1] = FREE
    u = (16 * 255 * 63) & 4095; e0 = ((u * u) >> 4) & (PL - 1); e1 = (((u * u) >> 4) + 255 * u) & (PL - 1)
    mem[e0 // C, 6, :, e0 % C] = 63; mem[e1 // C, 6, :, e1 % C] = 63
    nm[:, 6, T - 1] = e0; du[:, 6, T - 1] = FREE
    return pack({"mem": mem, "h": h, "val": val, "nm": nm, "du": du, "w": w, "kap": kap, "th": th})
def setup_inputs_meet(rng):
    p = parts(rng); b = np.array([0, 3, 4, 7]); e = np.array([1, 2, 5, 6]); gi = np.arange(8)[None, :, None]; s = np.arange(16)
    pool = p["nm"][0, :, 0].copy()
    nm = rng.permuted(np.broadcast_to(pool[None, :, None, :], (N, 8, T, 16)).copy(), axis=3); nm[:, 4] = pool[4]
    p["nm"][:, b] = nm[:, b]
    du = rng.integers(0, 3, (N, 8, T, 16)); dt = np.where(rng.random((N, 8, T, 16)) < 0.3, FREE, rng.integers(0, 2, (N, 8, T, 16)))
    du[:, e] = dt[:, e]; du[:, 4] = np.where((rng.random((N, T, 1)) < 0.2) & (s > S), FREE, 0); du[..., :S] = FREE; p["du"] = du
    pat = rng.integers(0, 4, (8, 6, 16)) * rng.choice(np.array([1, 3, 20]), (8, 1, 1))
    mem = pat[gi, rng.integers(0, 6, (N, 8, C))].transpose(0, 1, 3, 2)
    h = pat[gi, rng.integers(0, 6, (N, 8, T))].transpose(0, 1, 3, 2)
    val = pat[gi[..., None], rng.integers(0, 6, (N, 8, T, 16))].transpose(0, 1, 4, 2, 3)
    p["mem"][:, e] = mem[:, e]; p["h"][:, e] = h[:, e]; p["val"][:, e] = val[:, e]
    full = np.sum(np.max(pat, axis=1) - np.min(pat, axis=1), axis=1)
    off = rng.permuted(np.resize(np.array([0, 0, 1, -1, -3]), N * 4)).reshape(N, 4)
    p["th"][:, e] = np.maximum(full[e][None, :] + off, 0)
    p["th"][:, 0] = 0; p["th"][:, 4] = 0
    p["h"][:, 3] = p["h"][:1, 3, :, :1].copy(); p["w"][:, 3] = p["w"][:1, 3].copy(); p["kap"][:, 3] = p["kap"][:1, 3].copy()
    return pack(p)
def setup_inputs_spread(rng):
    p = parts(rng)
    p["mem"] = np.minimum((np.exp2(6 * rng.random((N, 8, 1, C))) * rng.random((N, 8, 16, C))).astype(np.int64), 63)
    p["h"] = np.minimum((np.exp2(6 * rng.random((N, 8, 1, T))) * rng.random((N, 8, 16, T))).astype(np.int64), 63)
    p["val"] = np.minimum((np.exp2(6 * rng.random((N, 8, 1, T, 16))) * rng.random((N, 8, 16, T, 16))).astype(np.int64), 63)
    p["w"] = np.minimum(np.exp2(8 * rng.random((N, 8, 16))).astype(np.int64), 255)
    p["th"] = rng.integers(0, 1009, (N, 8))
    du = np.where(rng.random((N, 8, T, 16)) < 0.5, rng.integers(0, 4, (N, 8, T, 16)), rng.integers(0, FREE + 1, (N, 8, T, 16))); du[..., :S] = FREE; p["du"] = du
    return pack(p)
def check_inputs(d):
    bad = []
    for k, lo, hi in RANGES:
        v = np.asarray(d[k]).astype(np.float64)
        if not (np.all(v >= lo) and np.all(v <= hi) and np.all(v == np.floor(v))): bad.append("range of " + k)
    du = np.asarray(d["due"]).astype(np.int64).reshape(N, 8, 16, T); nm = np.asarray(d["pnd"]).astype(np.int64).reshape(N, 8, 16, T)
    if np.any(du[:, :, :S] != FREE): bad.append("slots that start free")
    k = np.sort(np.where(du != FREE, nm, -1 - np.arange(16).reshape(1, 1, 16, 1)), axis=2)
    if np.any(k[:, :, 1:] == k[:, :, :-1]): bad.append("pending names of a thread differ")
    t = np.asarray(d["th"]).reshape(N, 8, 16)
    if np.any(t != t[:, :, :1]): bad.append("th alike in a group")
    return bad
def reference(mem, h, pnd, due, val, w, kap, th):
    whole = lambda a: a.astype(np.float32).astype(np.int64)
    mt = np.ascontiguousarray(whole(mem).reshape(N, 8, 16, C).transpose(1, 0, 3, 2)).reshape(8, PL, 16)
    hh = whole(h).reshape(N, 8, 16, T).transpose(0, 1, 3, 2)
    nm = pnd.astype(np.int64).reshape(N, 8, 16, T).transpose(0, 1, 3, 2).copy()
    du = due.astype(np.int64).reshape(N, 8, 16, T).transpose(0, 1, 3, 2).copy()
    vl = whole(val).reshape(N, 8, 16, T, 16).transpose(0, 1, 3, 4, 2).copy()
    ww = w.astype(np.int64).reshape(N, 8, 1, 16); kk = kap.astype(np.int64).reshape(N, 8, 1, 16); tt = th.astype(np.int64).reshape(N, 8, 16)[:, :, :1]
    A = np.zeros((N, 1, 1, 1), np.int64); s16 = np.arange(16); gi = np.arange(8).reshape(1, 8, 1, 1)
    for t in range(S):
        u = (np.sum(ww * hh, axis=3) & 4095)[..., None]
        z = ((u * u) >> 4) + kk * u + A
        a = np.where((s16 & 1) == 0, z, np.where(((z >> 3) & 1) == 1, nm + z, nm)) & (PL - 1)
        pend = du != FREE
        hit = (a[..., :, None] == nm[..., None, :]) & pend[..., None, :]
        x = np.where(np.any(hit, axis=4)[..., None], np.take_along_axis(vl, np.argmax(hit, axis=4)[..., None], 3), mt[gi, a])
        hi = np.max(x, axis=3); lo = np.min(x, axis=3); y = (hi + lo) >> 1
        score = np.sum(np.abs(x - hh[..., None, :]), axis=4)
        b = np.take_along_axis(a, np.argmax(score, axis=3)[..., None], 3)
        fence = np.sum(hi - lo, axis=3) >= tt
        same = (nm == b) & pend; had = np.any(same, axis=3)
        put = np.where(had[..., None], same, s16 == t) & ~fence[..., None]
        vl = np.where(put[..., None], y[..., None, :], vl); nm = np.where(put, b, nm)
        du[..., t] = np.where(~had & ~fence, t + 1 + (np.sum(y, axis=3) & DQ), du[..., t])
        sl = np.argmin(du, axis=3)[..., None]; least = np.take_along_axis(du, sl, 3)[..., 0]
        go = (least != FREE) & (fence | (least <= t))
        place = np.take_along_axis(nm, sl, 3)[..., 0]; value = np.take_along_axis(vl, sl[..., None], 3)[..., 0, :]
        du = np.where(go[..., None] & (s16 == sl), FREE, du)
        for g in range(8):
            m = go[:, g].reshape(-1); v = value[:, g].reshape(-1, 16)[m]
            first, at = np.unique(place[:, g].reshape(-1)[m], return_index=True)
            mt[g, first] = v[at]
        hh = np.abs(y - hh); A = (np.sum(fence, axis=(1, 2)) & 63).reshape(N, 1, 1, 1)
    bf = lambda e: np.ascontiguousarray(e).astype(np.float32).astype(BF)
    return {"ymem": bf(mt.reshape(8, N, C, 16).transpose(1, 0, 3, 2).reshape(N, 128, C)), "yh": bf(hh.transpose(0, 1, 3, 2).reshape(N, 128, T)),
            "ypnd": np.ascontiguousarray(nm.transpose(0, 1, 3, 2).reshape(N, 128, T)).astype(np.float32),
            "ydue": np.ascontiguousarray(du.transpose(0, 1, 3, 2).reshape(N, 128, T)).astype(np.float32),
            "yval": bf(vl.transpose(0, 1, 4, 2, 3).reshape(N, 128, 16 * T))}

@@ -1,0 +1,579 @@
+from concourse.mybir import dt, AluOpType as O, AxisListType, ActivationFunctionType as F
+from concourse.bass import DstId, RemoteDMATransfer
+
+NR, C, TH, STEPS = 8, 1024, 128, 3
+DUMP = NR * C
+VB = DUMP + TH
+VD = VB + 16 * TH
+WEND = VD + 16 * TH
+PW = 144
+MAGIC = 12582912.0
+POS = [2, 1, 0] + list(range(3, 16))
+NB = 48
+TA = TH - NB
+
+S, P = "sbuf", "psum"
+SCRATCH = {
+    "W": (S, [128, WEND], "bfloat16"), "vv": (S, [128, 16 * TH], "bfloat16"),
+    "hb": (S, [128, 256], "bfloat16"), "hp": (S, [128, 512], "bfloat16"),
+    "pI": (S, [128, 1], "int32"), "mI": (S, [128, 128], "int32"), "dI": (S, [128, 128], "int32"),
+    "ci1": (S, [128, 4], "int32"), "cols": (S, [128, 16], "float32"), "cT": (S, [128, 3], "float32"),
+    "md": (S, [128, 128], "int32"), "mm": (S, [128, 128], "int32"),
+    "I32": (S, [128, 128], "float32"), "Ib": (S, [128, 128], "bfloat16"), "nI": (S, [128, 128], "bfloat16"),
+    "I2": (S, [128, 128], "bfloat16"), "oddI": (S, [128, 128], "bfloat16"), "I8k": (S, [128, 128], "bfloat16"),
+    "B": (S, [128, 128], "bfloat16"), "nB": (S, [128, 128], "bfloat16"), "dl": (S, [128, 128], "bfloat16"),
+    "ofd": (S, [128, 128], "bfloat16"), "dc": (S, [128, 8], "float32"), "B1": (S, [128, 8], "bfloat16"),
+    "B16": (S, [128, 8], "bfloat16"), "dc128": (S, [128, 8], "bfloat16"), "Cl": (S, [128, 8], "bfloat16"),
+    "Cd": (S, [128, 8], "float32"), "rh2": (S, [128, 8], "float32"), "oh16": (S, [128, 16], "float32"),
+    "Sel": (S, [128, 2048], "bfloat16"), "KZ": (S, [128, 2048], "bfloat16"),
+    "TK": (S, [128, 128], "bfloat16"), "RS": (S, [128, 128], "float32"),
+    "xl": (S, [128, 8], "uint16"), "hl": (S, [128, 128], "uint16"),
+    "r1": (S, [128, 2048], "bfloat16"), "r2": (S, [128, 2048], "bfloat16"),
+    "tri": (S, [128, 512], "bfloat16"), "s0I": (S, [128, 1024], "int32"), "Sel0": (S, [128, 1024], "bfloat16"),
+    "nn": (S, [128, 8], "float32"), "on32": (S, [128, 128], "float32"), "t8k": (S, [128, 128], "bfloat16"),
+    "mh": (S, [128, 128], "bfloat16"), "ib": (S, [128, 128], "bfloat16"),
+    "wI": (S, [128, 1], "int32"), "kI": (S, [128, 1], "int32"), "tI": (S, [128, 1], "int32"),
+    "Wb": (S, [128, 128], "bfloat16"), "thd": (S, [128, 128], "float32"), "thE": (S, [128, 128], "float32"),
+    "th2": (S, [128, 128], "float32"),
+    "L1": (S, [128, 128], "int32"), "L2": (S, [128, 128], "int32"), "f1": (S, [128, 128], "float32"),
+    "f2": (S, [128, 128], "float32"),
+    "h0": (S, [128, 128], "bfloat16"), "h1": (S, [128, 128], "bfloat16"),
+    "nm": (S, [128, 128], "float32"), "pri": (S, [128, 128], "float32"),
+    "fr": (S, [128, 128], "bfloat16"), "qh": (S, [128, 128], "bfloat16"), "ql": (S, [128, 128], "bfloat16"),
+    "i1": (S, [128, 128], "int32"), "i2": (S, [128, 128], "int32"), "i3": (S, [128, 128], "int32"),
+    "i4": (S, [128, 128], "int32"), "i5": (S, [128, 128], "int32"), "i6": (S, [128, 128], "int32"),
+    "aI": (S, [128, 128], "int32"), "hit": (S, [128, 2048], "bfloat16"), "off": (S, [128, 128], "float32"),
+    "lst": (S, [128, 128], "uint16"), "hr": (S, [128, 2048], "bfloat16"), "d": (S, [128, 2048], "bfloat16"),
+    "ad": (S, [128, 2048], "bfloat16"), "sh": (S, [128, 2048], "bfloat16"), "sl": (S, [128, 2048], "bfloat16"),
+    "M0": (S, [128, 128], "float32"), "eq0": (S, [128, 128], "bfloat16"), "e1k": (S, [128, 128], "bfloat16"),
+    "PN": (S, [128, 128], "float32"), "N0": (S, [128, 128], "float32"), "n0c": (S, [128, 128], "float32"),
+    "sI": (S, [128, 128], "int32"), "sd": (S, [128, 128], "bfloat16"), "vl": (S, [128, 8], "uint16"),
+    "x1": (S, [128, 128], "bfloat16"), "x2": (S, [128, 128], "bfloat16"), "An": (S, [128, 128], "float32"),
+    "nh": (S, [128, 128], "bfloat16"), "nl": (S, [128, 128], "bfloat16"), "dab": (S, [128, 1024], "bfloat16"),
+    "eq": (S, [128, 1024], "bfloat16"), "y1": (S, [128, 128], "float32"), "yb": (S, [128, 128], "bfloat16"),
+    "ME": (S, [128, 128], "float32"), "oh": (S, [128, 128], "float32"), "no": (S, [128, 128], "float32"),
+    "PS": (S, [128, 128], "float32"), "SE": (S, [128, 128], "float32"), "go": (S, [128, 128], "bfloat16"),
+    "Fd": (S, [128, 128], "float32"),
+    "tg": (S, [128, 128], "float32"), "l1": (S, [128, 128], "float32"), "l2": (S, [128, 128], "float32"),
+    "sl16": (S, [128, 8], "uint16"), "sm": (S, [128, 64], "float32"), "smi": (S, [128, 20], "int32"),
+    "Ac": (S, [128, 4], "float32"), "rv": (S, [128, STEPS, NR, PW], "bfloat16"), "dcd": (S, [128, 64], "float32"),
+    "dL": (S, [128, 64], "uint16"),
+    "pn": (P, [128, 2048], "float32"), "pk": (P, [128, 512], "float32"), "p5": (P, [128, 512], "float32"),
+    "p6": (P, [128, 512], "float32"), "p7": (P, [128, 512], "float32"),
+}
+SEMAPHORES = ["qg", "qv", "qs", "qt", "ag", "lsA", "lsD", "hin", "hout"] + ["dr%d" % t for t in range(STEPS)] \
+    + ["rl%d" % t for t in range(STEPS)] + ["dm%d" % k for k in range(16)]
+
+
+def dst(topo, d, src):
+    rid, pid = topo.addr(d, src)
+    return DstId(rid=rid, pnc=pid)
+
+
+def bits(es):
+    m = 0
+    for e in es:
+        m |= 1 << e
+    return m
+
+
+def roles(T, topo, r):
+    me = T.cores[r]
+    near = [q for q in range(NR) if q != r and topo.may_write(me, T.cores[q])]
+    far = [q for q in range(NR) if q != r and q not in near]
+    chip = [c for c in topo.cores_of(me) if c != me]
+    car = [c for c in chip if topo.may_write(c, T.cores[far[0]])]
+    car = sorted(car, key=lambda c: (topo.die(c) != topo.die(me), c))
+    two = [c for c in chip if c not in car and topo.die(c) != topo.die(me)][0]
+    one = [c for c in car if topo.die(c) == topo.die(me)]
+    oth = [c for c in car if topo.die(c) != topo.die(me)]
+    relay = [(one[0], far[0::2]), (oth[0], far[1::2])]
+    return near, far, car, two, relay
+
+
+def helper_program(g, core, T, topo):
+    for r in range(NR):
+        me = T.cores[r]
+        if core not in topo.cores_of(me):
+            continue
+        near, far, car, two, relay = roles(T, topo, r)
+        loc = [e for e in topo.engines(me, two) if e not in topo.engines(me, T.cores[near[0]])]
+        n = 0
+        if core in car or core == two:
+            serve = far if core in car else near
+            buf = T.hb if core in car else T.hp
+            w = 256 if core in car else 512
+            lo = r * C + (car.index(core) * 256 if core in car else 512)
+            es = topo.engines(core, T.cores[serve[0]])
+            g.wait_ge(T.sem.hin, 2 if core in car else len(loc))
+            g.remote_dma_fused([RemoteDMATransfer(dst_ids=[dst(topo, T.cores[q], core) for q in serve], dma_engine_mask=bits(es),
+                                                  remote_sem=T.sem.ag, srcs=[buf[:, 0:w]],
+                                                  dsts=[T.W[:, lo:lo + w] for q in serve])], local_sem=T.sem.hout)
+            n += len(es)
+        for c, serve in relay:
+            if c != core:
+                continue
+            es = topo.engines(core, T.cores[serve[0]])
+            for t in range(STEPS):
+                g.wait_ge(T.sem["rl%d" % t], 4)
+                g.remote_dma_fused([RemoteDMATransfer(dst_ids=[dst(topo, T.cores[q], core) for q in serve], dma_engine_mask=bits(es),
+                                                      remote_sem=T.sem["dr%d" % t], srcs=[T.rv[:, t, r, :]],
+                                                      dsts=[T.rv[:, t, r, :] for q in serve])], local_sem=T.sem.hout)
+                n += len(es)
+        if n:
+            g.wait_ge(T.sem.hout, n)
+
+
+def rank_program(g, core, T, topo):
+    rank = T.rank_of(core)
+    if rank is None:
+        helper_program(g, core, T, topo)
+        return
+    near, far, car, two, relay = roles(T, topo, rank)
+
+    Q = {"g": g, "v": g.vector, "s": g.scalar, "t": g.tensor, "y": g.sync}
+    cnt, seen, log, ndma = {}, {q: {} for q in Q}, {}, [0]
+
+    def A(name, *idx):
+        ap = T[name]
+        shape = [int(x) for x in ap.shape][1:]
+        idx = idx + (slice(None),) * (len(shape) - len(idx))
+        lo = hi = 0
+        for n, i in zip(shape, idx):
+            if isinstance(i, slice):
+                a, b, st = i.indices(n)
+                last = a + (b - 1 - a) // st * st
+            else:
+                a = last = i
+            lo, hi = lo * n + a, hi * n + last
+        return {"ap": ap[(slice(None),) + idx], "n": name, "r": (lo, hi + 1), "ind": None}
+
+    def ind(win, offs):
+        return {"ap": win["ap"].indirect(offs["ap"]), "n": win["n"], "r": win["r"], "ind": offs}
+
+    def spans(v):
+        lo, hi = v["r"]
+        if v["n"] in SCRATCH and SCRATCH[v["n"]][0] == P:
+            return True, lo // 512 * 512, (hi + 511) // 512 * 512
+        return False, lo, hi
+
+    def need(q, v, write, acc):
+        ps, lo, hi = spans(v)
+        for e in log.get(v["n"], []):
+            if e["lo"] < hi and lo < e["hi"]:
+                same = e["q"] == q
+                if same and (ps and q == "t" or not e["w"]):
+                    continue
+                if e["w"] or write or ps and not same:
+                    acc.append(e["tok"])
+
+    def note(q, v, write, tok):
+        ps, lo, hi = spans(v)
+        L = log.setdefault(v["n"], [])
+        if write:
+            L[:] = [e for e in L if not (lo <= e["lo"] and e["hi"] <= hi and not ps)]
+        if ps:
+            L[:] = [e for e in L if not (e["q"] == q and e["w"] == write and e["lo"] == lo and e["hi"] == hi)]
+        L.append({"lo": lo, "hi": hi, "w": write, "q": q, "tok": tok})
+
+    def settle(q, toks):
+        best = {}
+        for s, n, snap in toks:
+            if seen[q].get(s, 0) < n and best.get(s, (0, 0))[0] < n:
+                best[s] = (n, snap)
+        for s in list(best):
+            if any(o != s and best[o][1].get(s, 0) >= best[s][0] for o in best):
+                del best[s]
+        for s in best:
+            n, snap = best[s]
+            Q[q].wait_ge(T.sem[s], n)
+            for k in snap:
+                seen[q][k] = max(seen[q].get(k, 0), snap[k])
+            seen[q][s] = n
+
+    calls = {"t": {"matmul": g.tensor.matmul, "transpose": g.tensor.transpose},
+             "s": {"activation": g.scalar.activation, "dma_start": g.scalar.dma_start},
+             "y": {"dma_start": g.sync.dma_start}, "g": {"iota": g.iota},
+             "v": {"tensor_copy": g.vector.tensor_copy, "tensor_tensor": g.vector.tensor_tensor, "memset": g.vector.memset,
+                   "tensor_scalar": g.vector.tensor_scalar, "tensor_tensor_scan": g.vector.tensor_tensor_scan}}
+
+    def E(q, meth, _pos=(), **kw):
+        wr, rd = [], []
+        for k, v in list(kw.items()) + [("ap", p) for p in _pos]:
+            if isinstance(v, dict):
+                (wr if k in ("out", "ap", "accum_out") else rd).append(v)
+                if v["ind"]:
+                    rd.append(v["ind"])
+        toks = []
+        for v in rd:
+            need(q, v, False, toks)
+        for v in wr:
+            need(q, v, True, toks)
+        settle(q, toks)
+        un = lambda v: v["ap"] if isinstance(v, dict) else v
+        ins = calls[q][meth](*[un(p) for p in _pos], **{k: un(v) for k, v in kw.items()})
+        if meth == "dma_start":
+            s, n = "dm%d" % ndma[0], 16
+            ndma[0] += 1
+            ins.then_inc(T.sem[s], 16)
+        else:
+            s = "q" + q
+            cnt[s] = n = cnt.get(s, 0) + 1
+            ins.then_inc(T.sem[s], 1)
+        tok = (s, n, dict(seen[q]))
+        dq = q if meth != "dma_start" else "dma"
+        for v in rd:
+            note(dq, v, False, tok)
+        for v in wr:
+            note(dq, v, True, tok)
+
+    def cp(out, in_):
+        E("v", "tensor_copy", out=out, in_=in_)
+
+    def tt(out, a, b, op):
+        E("v", "tensor_tensor", out=out, in0=a, in1=b, op=op)
+
+    def ts(out, a, s1, op0, s2=None, op1=None):
+        if op1 is None:
+            E("v", "tensor_scalar", out=out, in0=a, scalar1=s1, scalar2=None, op0=op0)
+        else:
+            E("v", "tensor_scalar", out=out, in0=a, scalar1=s1, scalar2=s2, op0=op0, op1=op1)
+
+    def act(out, in_, func=F.Identity, **kw):
+        E("s", "activation", out=out, in_=in_, func=func, **kw)
+
+    def mm(out, lhsT, rhs, start, stop):
+        E("t", "matmul", out=out, lhsT=lhsT, rhs=rhs, start=start, stop=stop)
+
+    def tr(out, in_):
+        E("t", "transpose", out=out, in_=in_, identity=A("I32"))
+
+    def group(out, pairs):
+        for k, (a, b) in enumerate(pairs):
+            mm(out, a, b, k == 0, k == len(pairs) - 1)
+
+    def scan(out, d0, d1, op0, op1, init):
+        E("v", "tensor_tensor_scan", out=out, data0=d0, data1=d1, initial=init, op0=op0, op1=op1)
+
+    def fill(v, x):
+        E("v", "memset", (v, x))
+
+    def ext(name):
+        return {"ap": T[name][:], "n": name, "r": (0, 1), "ind": None}
+
+    c = slice
+    COLS = ["pdf", "pmf", "pf", "odd", "ev8", "nbc", "key", "wf", "k16", "tf"]
+    K_ = lambda n: A("cols", c(COLS.index(n), COLS.index(n) + 1))
+    blk = lambda n, k: A(n, c(128 * k, 128 * k + 128))
+    spread = lambda n: ind(A(n), A("xl"))
+    H = ["h0", "h1"]
+
+    def slots(t):
+        return [s for s in range(16) if s >= STEPS or s < t]
+
+    E("y", "dma_start", out=A("W", c(rank * C, rank * C + C)), in_=ext("mem"))
+    E("s", "dma_start", out=A("L1"), in_=ext("pnd"))
+    E("s", "dma_start", out=A("L2"), in_=ext("due"))
+    E("y", "dma_start", out=A("h0"), in_=ext("h"))
+    E("s", "dma_start", out=A("wI"), in_=ext("w"))
+    E("y", "dma_start", out=A("kI"), in_=ext("kap"))
+    E("y", "dma_start", out=A("tI"), in_=ext("th"))
+    E("y", "dma_start", out=A("vv"), in_=ext("val"))
+    E("g", "iota", out=A("pI"), pattern=[[0, 1]], base=0, channel_multiplier=1)
+    E("g", "iota", out=A("mI"), pattern=[[1, 128]], base=0, channel_multiplier=0)
+    E("g", "iota", out=A("dI"), pattern=[[-1, 128]], base=0, channel_multiplier=1)
+
+    toks = []
+    own = A("W", c(rank * C, rank * C + C))
+    need("g", own, False, toks)
+    settle("g", toks)
+    sub = lambda a, b: T.W[:, rank * C + a:rank * C + b]
+    e8 = topo.engines(core, T.cores[near[0]])
+    loc = [e for e in topo.engines(core, two) if e not in e8]
+    g.remote_dma_fused([RemoteDMATransfer(dst_ids=[dst(topo, k, core)], dma_engine_mask=bits(loc[2 * j:2 * j + 2]), remote_sem=T.sem.hin,
+                                          srcs=[sub(256 * j, 256 * j + 256)], dsts=[T.hb[:, 0:256]]) for j, k in enumerate(car)],
+                       local_sem=T.sem.lsA)
+    g.remote_dma_fused([RemoteDMATransfer(dst_ids=[dst(topo, two, core)], dma_engine_mask=bits(loc), remote_sem=T.sem.hin,
+                                          srcs=[sub(512, 1024)], dsts=[T.hp[:, 0:512]]),
+                        RemoteDMATransfer(dst_ids=[dst(topo, T.cores[q], core) for q in near], dma_engine_mask=bits(e8), remote_sem=T.sem.ag,
+                                          srcs=[sub(0, 512)], dsts=[sub(0, 512) for q in near])], local_sem=T.sem.lsA)
+    nown = 2 * len(car) + len(loc) + len(e8)
+    note("rem", own, False, ("lsA", nown, {}))
+    nag = len(e8) * (2 * len(near) + 4 * len(far))
+    for q in range(NR):
+        if q != rank:
+            note("rem", A("W", c(q * C, q * C + C)), True, ("ag", nag, {}))
+    small = {"channel_multiplier": 0, "allow_small_or_imprecise_dtypes": True}
+    E("g", "iota", out=A("RS"), pattern=[[0, 8], [32767, 16]], base=0, **small)
+    E("g", "iota", out=A("s0I"), pattern=[[16, 8], [0, 128]], base=0, channel_multiplier=-1)
+    E("g", "iota", out=A("TK"), pattern=[[0, 8], [-1, 16]], base=15, **small)
+    E("g", "iota", out=A("r1"), pattern=[[0, 128], [256, 16]], base=-128, **small)
+    E("g", "iota", out=A("r2"), pattern=[[0, 128], [-256, 16]], base=128, **small)
+
+    cI = lambda k: A("ci1", c(k, k + 1))
+    ts(A("I32"), A("dI"), 0, O.is_equal)
+    ts(A("Ib"), A("dI"), 0, O.is_equal)
+    ts(cI(0), A("pI"), 4, O.arith_shift_right)
+    ts(cI(1), A("pI"), 15, O.bitwise_and)
+    ts(cI(2), A("pI"), 1, O.bitwise_and)
+    ts(A("md"), A("mI"), 4, O.arith_shift_right)
+    cp(K_("pdf"), cI(0))
+    cp(K_("pmf"), cI(1))
+    cp(K_("odd"), cI(2))
+    cp(K_("pf"), A("pI"))
+    ts(A("B"), A("md"), K_("pdf"), O.is_equal)
+    ts(A("oh16"), A("mI", c(0, 16)), K_("pmf"), O.is_equal)
+    ts(K_("key"), A("oh16", c(0, 1)), 14.0, O.mult, 1008.0, O.add)
+    tt(K_("key"), K_("key"), K_("pmf"), O.subtract)
+    fill(A("t8k"), 8192.0)
+    cp(A("f1"), A("L1"))
+    ts(A("f2"), A("L2"), -32.0, O.mult, K_("key"), O.add)
+    tr(A("p5", c(0, 128)), A("f1"))
+    tr(A("p6", c(0, 128)), A("f2"))
+    act(A("I8k"), A("Ib"), scale=8192.0)
+    act(A("nI"), A("Ib"), scale=-1.0)
+    act(A("nm"), A("p5", c(0, 128)))
+    act(A("pri"), A("p6", c(0, 128)))
+    cp(K_("wf"), A("wI"))
+    ts(A("Wb"), A("B"), K_("wf"), O.mult)
+    for s in range(3, 16):
+        ts(blk("Sel", s), A("B"), A("oh16", c(s, s + 1)), O.mult)
+    ts(K_("k16"), A("kI"), 16.0, O.mult)
+    ts(K_("ev8"), K_("odd"), -8.0, O.mult, 8.0, O.add)
+    ts(A("oddI"), A("Ib"), K_("odd"), O.mult)
+    ts(A("ib"), A("mI"), -128.0, O.add)
+
+    def prepare(t, h):
+        L = slots(t)
+        mm(A("p6", c(384, 512)), A("Wb"), A(h), True, True)
+        act(A("fr"), A("pri"), F.Sign, scale=-1.0, bias=32.5)
+        group(A("p7", c(0, 128)), [(A("nm"), A("I32")), (A("Ib"), A("t8k")), (A("fr"), A("I8k"))])
+        act(A("qh"), A("p7", c(0, 128)))
+        scan(A("M0"), A("RS"), A("pri"), O.min, O.max, 0.0)
+        tt(A("eq0"), spread("M0"), A("pri"), O.is_equal)
+        tt(A("ql"), A("p7", c(0, 128)), A("qh"), O.subtract)
+        group(A("p6", c(0, 128)), [(A("oddI"), A("qh")), (A("oddI"), A("ql"))])
+        for j, s in enumerate(L):
+            group(blk("pn", j), [(blk("Sel", s), A("qh")), (blk("Sel", s), A("ql"))])
+        tt(A("PN"), A("eq0"), A("nm"), O.mult)
+        ts(A("sI"), spread("M0"), -1.0, O.mult, 1024.0, O.add)
+        scan(A("N0"), A("RS"), A("PN"), O.min, O.max, 0.0)
+        ts(A("sI"), A("sI"), 15, O.bitwise_and)
+        act(A("n0c"), spread("N0"))
+        tr(A("p7", c(256, 384)), A("n0c"))
+        act(A("nh"), A("p7", c(256, 384)))
+        group(A("p7", c(256, 384)), [(A("n0c"), A("I32")), (A("nI"), A("nh"))])
+        act(A("An"), spread("N0"), bias=K_("nbc"))
+        act(A("nl"), A("p7", c(256, 384)))
+        act(A("nn"), A("N0", c(15, 128, 16)), scale=-1.0)
+        act(A("e1k"), A("eq0"), scale=1024.0)
+        act(A("x1"), spread("M0"), F.Relu, scale=-2048.0, bias=2048.0 * 33)
+        act(A("x2"), spread("M0"), F.Relu, scale=2048.0, bias=-2048.0 * (1024 - 32 * (t + 1)))
+        act(A("hr"), ind(A(h), A("hl")))
+        tt(A("sd"), A("sI"), A("dl"), O.mult)
+        group(A("pk", c(480, 488)), [(A("sd"), A("dc128")), (A("Ib"), A("Cl"))])
+        cp(A("i1"), A("p6", c(384, 512)))
+        ts(A("i2"), A("i1"), 4095, O.bitwise_and)
+        ts(A("i3"), A("i2"), K_("k16"), O.add)
+        tt(A("i4"), A("i2"), A("i3"), O.mult)
+        ts(A("i5"), A("i4"), 4, O.arith_shift_right)
+        if t:
+            ts(A("i6"), A("i5"), K_("odd"), O.mult, A("Ac", c(1, 2)), O.add)
+            ts(A("i1"), A("i5"), A("Ac", c(0, 1)), O.add)
+            z = "i1"
+        else:
+            ts(A("i6"), A("i5"), K_("odd"), O.mult, K_("ev8"), O.add)
+            z = "i5"
+        ts(A("i3"), A("i6"), 3, O.arith_shift_right, 1, O.bitwise_and)
+        tt(A("i4"), A(z), A("i3"), O.mult)
+        tt(A("i6"), A("i4"), A("p6", c(0, 128)), O.add)
+        ts(A("aI"), A("i6"), 8191, O.bitwise_and)
+        for j in range(len(L)):
+            tt(blk("hit", j), A("aI"), blk("pn", j), O.is_equal)
+        group(A("p5", c(0, 128)), [(A("Ib"), A("ib"))] + [(blk("KZ", s), blk("hit", j)) for j, s in enumerate(L)])
+        tt(A("off"), A("aI"), A("p5", c(0, 128)), O.max)
+        cp(A("lst"), A("off"))
+        tr(A("p6", c(128, 256)), A("off"))
+        for b in range(2):
+            mm(A("pn", c(512 * b, 512 * b + 512)), A("Ib"), A("tri"), True, False)
+            for k in range(4 * b, 4 * b + 4):
+                mm(blk("pn", k), blk("Sel0", k), A("nh"), False, False)
+                mm(blk("pn", k), blk("Sel0", k), A("nl"), False, k == 4 * b + 3)
+        for k in range(8):
+            act(blk("dab", k), blk("pn", k), F.Abs, bias=A("nn", c(k, k + 1)))
+        for b in range(2):
+            half = c(512 * b, 512 * b + 512)
+            act(A("eq", half), A("dab", half), F.Relu, scale=-1.0, bias=1.0)
+
+    def reads(t, h):
+        win = A("W", c(0, VD))
+        A2 = TA // 4 * 2
+        act(A("d", c(16 * TA, 2048)), ind(win, A("lst", c(TA, TH))))
+        for a, b in ((0, A2), (A2, TA)):
+            part = c(16 * a, 16 * b)
+            E("v", "tensor_tensor", out=A("d", part), in0=ind(win, A("lst", c(a, b))), in1=A("hr", part), op=O.subtract)
+        cp(A("vl"), A("pk", c(480, 488)))
+        for a in range(TA, TH, 32):
+            b = min(a + 32, TH)
+            out = A("pn", c(1024 + 16 * (a - TA), 1024 + 16 * (b - TA)))
+            mm(out, A("nI"), A("hr", c(16 * a, 16 * b)), True, False)
+            mm(out, A("Ib"), A("d", c(16 * a, 16 * b)), False, True)
+        for a, b in ((0, A2), (A2, TA)):
+            act(A("ad", c(16 * a, 16 * b)), A("d", c(16 * a, 16 * b)), F.Abs)
+        act(A("ad", c(16 * TA, 2048)), A("pn", c(1024, 1024 + 16 * NB)), F.Abs)
+        key = A("pk", c(0, 128))
+        mm(key, A("Ib"), A("TK"), True, False)
+        for k in range(16):
+            mm(A("pk", c(k, 128, 16)), A("ad", c(k, None, 16)), A("B16"), False, k == 15)
+        scan(A("sh"), A("r1"), A("d"), O.min, O.max, -128.0)
+        scan(A("sl"), A("r2"), A("d"), O.max, O.min, 128.0)
+        hi, lo = A("sh", c(15, None, 16)), A("sl", c(15, None, 16))
+        group(A("p5", c(128, 256)), [(A("nI"), A("x1")), (A("Ib"), A("x2")), (hi, A("B")), (lo, A("nB"))])
+        group(A("p5", c(0, 128)), [(hi, A("B")), (lo, A("nB"))])
+        mm(A("pn", c(0, 128)), A("Ib"), A("mh"), True, False)
+        mm(A("pn", c(0, TA)), A("I2"), A(h, c(0, TA)), False, False)
+        mm(A("pn", c(0, 128)), A("Ib"), hi, False, False)
+        mm(A("pn", c(0, 128)), A("Ib"), lo, False, True)
+        act(A("y1"), A("pn", c(0, 128)), scale=0.5, bias=MAGIC)
+        act(A("yb"), A("y1"), bias=-MAGIC)
+        tt(A("go"), A("p5", c(128, 256)), A("thE"), O.is_ge)
+        tt(A("Fd"), A("p5", c(0, 128)), A("th2"), O.is_ge)
+        mm(A("p7", c(0, 128)), A("Ib"), A("ofd"), True, False)
+        for k in range(8):
+            mm(A("p7", c(16 * k, 16 * k + 16)), blk("eq", k), A("go", c(16 * k, 16 * k + 16)), False, k == 7)
+        scan(A("ME"), A("RS"), key, O.min, O.max, 0.0)
+        tt(A("oh"), key, A("ME"), O.is_equal)
+        tt(A("no"), key, A("ME"), O.not_equal)
+        tt(A("PS"), A("oh"), A("p6", c(128, 256)), O.mult)
+        scan(A("SE"), A("no"), A("PS"), O.mult, O.add, 0.0)
+        ts(A("tg"), spread("SE"), -float(VB), O.add, A("cT", c(t, t + 1)), O.max)
+        tt(A("l1"), A("tg"), A("dl"), O.mult)
+        group(A("pn", c(512, 520)), [(A("Fd"), A("rh2")), (A("l1"), A("dc"))])
+        tt(A("l2"), A("go"), A("p7", c(0, 128)), O.is_gt)
+        cp(A("sl16"), A("pn", c(512, 520)))
+        tt(A("l2"), A("l2"), A("An"), O.mult)
+        group(A("pn", c(1024, 1032)), [(A("I32"), A("Cd")), (A("l2"), A("dc"))])
+        E("v", "tensor_copy", out=ind(A("W", c(VB, WEND)), A("sl16")), in_=A("yb"))
+        act(A("rv", t, rank, c(128, 136)), A("pn", c(1024, 1032)))
+        E("v", "tensor_copy", out=A("rv", t, rank, c(0, 128)), in_=ind(A("W", c(VB, WEND)), A("vl")))
+        tt(A("rv", t, rank, c(136, 144)), A("pn", c(1024, 1032)), A("rv", t, rank, c(128, 136)), O.subtract)
+        toks = []
+        need("g", A("rv", t, rank), False, toks)
+        settle("g", toks)
+        piece = T.rv[:, t, rank, :]
+        sends = [RemoteDMATransfer(dst_ids=[dst(topo, k, core)], dma_engine_mask=bits(loc[4 * j:4 * j + 4]), remote_sem=T.sem["rl%d" % t],
+                                   srcs=[piece], dsts=[piece]) for j, (k, _) in enumerate(relay)]
+        sends.append(RemoteDMATransfer(dst_ids=[dst(topo, T.cores[q], core) for q in near], dma_engine_mask=bits(e8),
+                                       remote_sem=T.sem["dr%d" % t], srcs=[piece], dsts=[piece for q in near]))
+        g.remote_dma_fused(sends, local_sem=T.sem.lsD)
+        for q in range(NR):
+            if q != rank:
+                note("rem", A("rv", t, q), True, ("dr%d" % t, len(e8) * (NR - 1), {}))
+
+    def update(t, h, hn):
+        group(A("pn", c(0, 128)), [(A("Ib"), A("yb")), (A("nI"), A(h))])
+        act(A(hn), A("pn", c(0, 128)), F.Abs)
+        mm(A("pn", c(1536, 1544)), A("yb"), A("B1"), True, True)
+        if t < STEPS - 1:
+            mm(A("pn", c(512, 640)), A("on32"), A("Fd"), True, True)
+            act(A("f1"), A("pn", c(512, 640)), accum_out=A("Ac", c(2, 3)))
+        s = lambda k: A("sm", c(8 * k, 8 * k + 8))
+        si = lambda k: A("smi", c(8 * k, 8 * k + 8))
+        col = lambda n, k: A(n, c(k, 128, 16))
+        tt(A("f2"), A("go"), A("e1k"), O.mult)
+        ts(s(0), col("SE", 15), float(VB), O.is_lt)
+        tt(s(1), col("p5", 15), col("thE", 15), O.is_lt)
+        cp(si(0), A("pn", c(1536, 1544)))
+        tt(s(3), col("SE", 15), col("nm", t), O.subtract)
+        tt(s(2), s(0), s(1), O.mult)
+        ts(si(1), si(0), 7, O.bitwise_and)
+        tt(s(3), s(3), s(2), O.mult)
+        ts(s(4), si(1), -32.0, O.mult, 960.0 - 32 * t, O.add)
+        tt(col("nm", t), col("nm", t), s(3), O.add)
+        tt(s(4), s(4), s(2), O.mult)
+        tt(A("pri"), A("pri"), A("f2"), O.subtract)
+        tt(col("pri", t), col("pri", t), s(4), O.add)
+        if t < STEPS - 1:
+            ai = lambda k: A("smi", c(16 + k, 17 + k))
+            cp(ai(0), A("Ac", c(2, 3)))
+            ts(ai(1), ai(0), 63, O.bitwise_and)
+            cp(A("Ac", c(0, 1)), ai(1))
+            ts(A("Ac", c(1, 2)), ai(1), K_("odd"), O.mult, K_("ev8"), O.add)
+
+    def drains(t):
+        tt(A("dcd"), A("rv", t, c(None), c(128, 136)), A("rv", t, c(None), c(136, 144)), O.add)
+        cp(A("dL"), A("dcd"))
+        for q in range(NR - 1, -1, -1):
+            E("v", "tensor_copy", out=ind(A("W", c(0, VB)), A("dL", c(8 * q, 8 * q + 8))), in_=A("rv", t, q, c(0, 128)))
+
+    for s in range(3, 16):
+        act(blk("KZ", s), A("Ib"), scale=float(VB + 128 * (POS[s] + 1)))
+    ts(A("xl"), A("mI", c(0, 8)), 16.0, O.mult, 15.0, O.add)
+    cp(A("hl"), A("mI"))
+    ts(A("mm"), A("mI"), 15, O.bitwise_and)
+    ts(A("dl"), A("mm"), K_("pmf"), O.is_equal)
+    ts(A("dc"), A("mI", c(0, 8)), K_("pdf"), O.is_equal)
+    ts(A("dc128"), A("dc"), 128.0, O.mult)
+    ts(A("Cl"), A("mI", c(0, 8)), 16.0, O.mult, K_("pmf"), O.add)
+    ts(K_("nbc"), K_("pf"), -1.0, O.mult, -float(DUMP), O.add)
+    for k in range(4):
+        ts(blk("tri", k), A("dI"), 0, O.is_ge, 16384.0, O.mult)
+    ts(A("Sel0"), A("s0I"), 0, O.is_equal)
+    prepare(0, H[0])
+    for k in range(3):
+        ts(A("cT", c(k, k + 1)), K_("pf"), 128.0 * POS[k], O.add)
+    ts(A("ofd"), A("mm"), K_("pmf"), O.not_equal, 4.0, O.mult)
+    ts(A("B1"), A("dc"), 1.0, O.mult)
+    ts(A("B16"), A("dc"), 16.0, O.mult)
+    ts(A("Cd"), A("Cl"), float(DUMP), O.add)
+    ts(A("rh2"), A("dc"), 2048.0, O.mult)
+    fill(A("W", c(DUMP, VB)), 0.0)
+    fill(A("W", c(VD, WEND)), 0.0)
+    fill(A("on32"), 1.0)
+    fill(A("mh"), -0.5)
+    cp(K_("tf"), A("tI"))
+    ts(A("thd"), A("I32"), K_("tf"), O.mult)
+    mm(A("p5", c(256, 384)), A("on32"), A("thd"), True, True)
+    vslot = lambda s: A("W", c(VB + 128 * POS[s], VB + 128 * POS[s] + 128))
+    for s in range(16):
+        if s % 2:
+            act(vslot(s), A("vv", c(s, None, 16)))
+        else:
+            cp(vslot(s), A("vv", c(s, None, 16)))
+    act(A("thE"), A("p5", c(256, 384)))
+    ts(A("f1"), A("ofd"), 1024.0, O.mult)
+    tt(A("th2"), A("thE"), A("f1"), O.add)
+    act(A("nB"), A("B"), scale=-1.0)
+    act(A("I2"), A("Ib"), scale=2.0)
+    for t in range(STEPS):
+        h, hn = H[t % 2], H[1 - t % 2]
+        reads(t, h)
+        if t == 0:
+            for s in (0, 1):
+                ts(blk("Sel", s), A("B"), A("oh16", c(s, s + 1)), O.mult)
+                act(blk("KZ", s), A("Ib"), scale=float(VB + 128 * (POS[s] + 1)))
+        update(t, h, hn)
+        if t < STEPS - 1:
+            prepare(t + 1, hn)
+        else:
+            E("y", "dma_start", out=ext("yh"), in_=A(hn))
+            for s in range(16):
+                act(A("vv", c(s, None, 16)), vslot(s))
+            tr(A("pn", c(0, 128)), A("nm"))
+            ts(A("sI"), A("pri"), -0.03125, O.mult, 32.0 - 31.0 / 64, O.add)
+            ts(A("off"), A("sI"), 31.0, O.min)
+            tr(A("pn", c(512, 640)), A("off"))
+            cp(A("f1"), A("pn", c(0, 128)))
+            cp(A("l1"), A("pn", c(512, 640)))
+            E("y", "dma_start", out=ext("ypnd"), in_=A("f1"))
+            E("y", "dma_start", out=ext("ydue"), in_=A("l1"))
+            E("y", "dma_start", out=ext("yval"), in_=A("vv"))
+        drains(t)
+    E("y", "dma_start", out=ext("ymem"), in_=A("W", c(rank * C, rank * C + C)))
+    g.wait_ge(T.sem.lsD, STEPS * (8 + len(e8)))
+    for k in range(ndma[0]):
+        if not any(seen[q].get("dm%d" % k, 0) for q in Q):
+            g.sync.wait_ge(T.sem["dm%d" % k], 16)
+    for q in "gvst":
+        if cnt.get("q" + q, 0) > max(seen[o].get("q" + q, 0) for o in Q):
+            g.sync.wait_ge(T.sem["q" + q], cnt["q" + q])

@@ -15,21 +15,23 @@ TA = TH - NB
 S, P = "sbuf", "psum"
 SCRATCH = {
     "W": (S, [128, WEND], "bfloat16"), "vv": (S, [128, 16 * TH], "bfloat16"),
-    "hb": (S, [128, 256], "bfloat16"), "hp": (S, [128, 512], "bfloat16"),
+    "hb": (S, [128, 256], "bfloat16"),
     "pI": (S, [128, 1], "int32"), "mI": (S, [128, 128], "int32"), "dI": (S, [128, 128], "int32"),
     "ci1": (S, [128, 4], "int32"), "cols": (S, [128, 16], "float32"), "cT": (S, [128, 3], "float32"),
     "md": (S, [128, 128], "int32"), "mm": (S, [128, 128], "int32"),
     "I32": (S, [128, 128], "float32"), "Ib": (S, [128, 128], "bfloat16"), "nI": (S, [128, 128], "bfloat16"),
     "I2": (S, [128, 128], "bfloat16"), "oddI": (S, [128, 128], "bfloat16"), "I8k": (S, [128, 128], "bfloat16"),
+    "I16k": (S, [128, 128], "bfloat16"),
     "B": (S, [128, 128], "bfloat16"), "nB": (S, [128, 128], "bfloat16"), "dl": (S, [128, 128], "bfloat16"),
-    "ofd": (S, [128, 128], "bfloat16"), "dc": (S, [128, 8], "float32"), "B1": (S, [128, 8], "bfloat16"),
+    "ofd": (S, [128, 128], "bfloat16"), "dc": (S, [128, 8], "float32"), "B8th": (S, [128, 8], "bfloat16"),
+    "Bm32": (S, [128, 8], "bfloat16"), "c716": (S, [128, 8], "bfloat16"), "c960": (S, [128, 24], "bfloat16"),
     "B16": (S, [128, 8], "bfloat16"), "dc128": (S, [128, 8], "bfloat16"), "Cl": (S, [128, 8], "bfloat16"),
     "Cd": (S, [128, 8], "float32"), "rh2": (S, [128, 8], "float32"), "oh16": (S, [128, 16], "float32"),
     "Sel": (S, [128, 2048], "bfloat16"), "KZ": (S, [128, 2048], "bfloat16"),
     "TK": (S, [128, 128], "bfloat16"), "RS": (S, [128, 128], "float32"),
     "xl": (S, [128, 8], "uint16"), "hl": (S, [128, 128], "uint16"),
     "r1": (S, [128, 2048], "bfloat16"), "r2": (S, [128, 2048], "bfloat16"),
-    "tri": (S, [128, 512], "bfloat16"), "s0I": (S, [128, 1024], "int32"), "Sel0": (S, [128, 1024], "bfloat16"),
+    "tri": (S, [128, 128], "bfloat16"), "on1": (S, [128, 1024], "bfloat16"), "Sel0": (S, [128, 1024], "bfloat16"),
     "nn": (S, [128, 8], "float32"), "on32": (S, [128, 128], "float32"), "t8k": (S, [128, 128], "bfloat16"),
     "mh": (S, [128, 128], "bfloat16"), "ib": (S, [128, 128], "bfloat16"),
     "wI": (S, [128, 1], "int32"), "kI": (S, [128, 1], "int32"), "tI": (S, [128, 1], "int32"),
@@ -46,17 +48,17 @@ SCRATCH = {
     "lst": (S, [128, 128], "uint16"), "hr": (S, [128, 2048], "bfloat16"), "d": (S, [128, 2048], "bfloat16"),
     "ad": (S, [128, 2048], "bfloat16"), "sh": (S, [128, 2048], "bfloat16"), "sl": (S, [128, 2048], "bfloat16"),
     "M0": (S, [128, 128], "float32"), "eq0": (S, [128, 128], "bfloat16"), "e1k": (S, [128, 128], "bfloat16"),
-    "PN": (S, [128, 128], "float32"), "N0": (S, [128, 128], "float32"), "n0c": (S, [128, 128], "float32"),
+    "N0": (S, [128, 128], "float32"), "n0c": (S, [128, 128], "float32"),
     "sI": (S, [128, 128], "int32"), "sd": (S, [128, 128], "bfloat16"), "vl": (S, [128, 8], "uint16"),
     "x1": (S, [128, 128], "bfloat16"), "x2": (S, [128, 128], "bfloat16"), "An": (S, [128, 128], "float32"),
     "nh": (S, [128, 128], "bfloat16"), "nl": (S, [128, 128], "bfloat16"), "dab": (S, [128, 1024], "bfloat16"),
     "eq": (S, [128, 1024], "bfloat16"), "y1": (S, [128, 128], "float32"), "yb": (S, [128, 128], "bfloat16"),
     "ME": (S, [128, 128], "float32"), "oh": (S, [128, 128], "float32"), "no": (S, [128, 128], "float32"),
     "PS": (S, [128, 128], "float32"), "SE": (S, [128, 128], "float32"), "go": (S, [128, 128], "bfloat16"),
-    "Fd": (S, [128, 128], "float32"),
+    "Fd": (S, [128, 128], "float32"), "r8": (S, [128, 16], "float32"),
     "tg": (S, [128, 128], "float32"), "l1": (S, [128, 128], "float32"), "l2": (S, [128, 128], "float32"),
-    "sl16": (S, [128, 8], "uint16"), "sm": (S, [128, 64], "float32"), "smi": (S, [128, 20], "int32"),
-    "Ac": (S, [128, 4], "float32"), "rv": (S, [128, STEPS, NR, PW], "bfloat16"), "dcd": (S, [128, 64], "float32"),
+    "sl16": (S, [128, 8], "uint16"), "sm": (S, [128, 64], "float32"),
+    "Ac": (S, [128, 8], "float32"), "rv": (S, [128, STEPS, NR, PW], "bfloat16"), "dcd": (S, [128, 64], "float32"),
     "dL": (S, [128, 64], "uint16"),
     "pn": (P, [128, 2048], "float32"), "pk": (P, [128, 512], "float32"), "p5": (P, [128, 512], "float32"),
     "p6": (P, [128, 512], "float32"), "p7": (P, [128, 512], "float32"),
@@ -84,11 +86,10 @@ def roles(T, topo, r):
     chip = [c for c in topo.cores_of(me) if c != me]
     car = [c for c in chip if topo.may_write(c, T.cores[far[0]])]
     car = sorted(car, key=lambda c: (topo.die(c) != topo.die(me), c))
-    two = [c for c in chip if c not in car and topo.die(c) != topo.die(me)][0]
-    one = [c for c in car if topo.die(c) == topo.die(me)]
-    oth = [c for c in car if topo.die(c) != topo.die(me)]
-    relay = [(one[0], far[0::2]), (oth[0], far[1::2])]
-    return near, far, car, two, relay
+    plain = [c for c in chip if c not in car]
+    a = sum(q < r for q in near)
+    relay = [(car[(a + b) % 2 * 2 + b // 2], q) for b, q in enumerate(far)]
+    return near, far, car, plain, relay
 
 
 def helper_program(g, core, T, topo):
@@ -96,29 +97,26 @@ def helper_program(g, core, T, topo):
         me = T.cores[r]
         if core not in topo.cores_of(me):
             continue
-        near, far, car, two, relay = roles(T, topo, r)
-        loc = [e for e in topo.engines(me, two) if e not in topo.engines(me, T.cores[near[0]])]
+        near, far, car, plain, relay = roles(T, topo, r)
         n = 0
-        if core in car or core == two:
+        if core in car or core in plain:
             serve = far if core in car else near
-            buf = T.hb if core in car else T.hp
-            w = 256 if core in car else 512
-            lo = r * C + (car.index(core) * 256 if core in car else 512)
+            lo = r * C + 256 * (car.index(core) if core in car else 1 + plain.index(core))
             es = topo.engines(core, T.cores[serve[0]])
-            g.wait_ge(T.sem.hin, 2 if core in car else len(loc))
+            g.wait_ge(T.sem.hin, 2)
             g.remote_dma_fused([RemoteDMATransfer(dst_ids=[dst(topo, T.cores[q], core) for q in serve], dma_engine_mask=bits(es),
-                                                  remote_sem=T.sem.ag, srcs=[buf[:, 0:w]],
-                                                  dsts=[T.W[:, lo:lo + w] for q in serve])], local_sem=T.sem.hout)
+                                                  remote_sem=T.sem.ag, srcs=[T.hb[:]],
+                                                  dsts=[T.W[:, lo:lo + 256] for q in serve])], local_sem=T.sem.hout)
             n += len(es)
-        for c, serve in relay:
+        for c, q in relay:
             if c != core:
                 continue
-            es = topo.engines(core, T.cores[serve[0]])
+            es = topo.engines(core, T.cores[q])
             for t in range(STEPS):
                 g.wait_ge(T.sem["rl%d" % t], 4)
-                g.remote_dma_fused([RemoteDMATransfer(dst_ids=[dst(topo, T.cores[q], core) for q in serve], dma_engine_mask=bits(es),
+                g.remote_dma_fused([RemoteDMATransfer(dst_ids=[dst(topo, T.cores[q], core)], dma_engine_mask=bits(es),
                                                       remote_sem=T.sem["dr%d" % t], srcs=[T.rv[:, t, r, :]],
-                                                      dsts=[T.rv[:, t, r, :] for q in serve])], local_sem=T.sem.hout)
+                                                      dsts=[T.rv[:, t, r, :]])], local_sem=T.sem.hout)
                 n += len(es)
         if n:
             g.wait_ge(T.sem.hout, n)
@@ -129,7 +127,7 @@ def rank_program(g, core, T, topo):
     if rank is None:
         helper_program(g, core, T, topo)
         return
-    near, far, car, two, relay = roles(T, topo, rank)
+    near, far, car, plain, relay = roles(T, topo, rank)
 
     Q = {"g": g, "v": g.vector, "s": g.scalar, "t": g.tensor, "y": g.sync}
     cnt, seen, log, ndma = {}, {q: {} for q in Q}, {}, [0]
@@ -193,7 +191,7 @@ def rank_program(g, core, T, topo):
 
     calls = {"t": {"matmul": g.tensor.matmul, "transpose": g.tensor.transpose},
              "s": {"activation": g.scalar.activation, "dma_start": g.scalar.dma_start},
-             "y": {"dma_start": g.sync.dma_start}, "g": {"iota": g.iota},
+             "y": {"dma_start": g.sync.dma_start}, "g": {"iota": g.iota, "affine_select": g.affine_select},
              "v": {"tensor_copy": g.vector.tensor_copy, "tensor_tensor": g.vector.tensor_tensor, "memset": g.vector.memset,
                    "tensor_scalar": g.vector.tensor_scalar, "tensor_tensor_scan": g.vector.tensor_tensor_scan}}
 
@@ -266,6 +264,7 @@ def rank_program(g, core, T, topo):
     K_ = lambda n: A("cols", c(COLS.index(n), COLS.index(n) + 1))
     blk = lambda n, k: A(n, c(128 * k, 128 * k + 128))
     spread = lambda n: ind(A(n), A("xl"))
+    vslot = lambda s: A("W", c(VB + 128 * POS[s], VB + 128 * POS[s] + 128))
     H = ["h0", "h1"]
 
     def slots(t):
@@ -278,7 +277,6 @@ def rank_program(g, core, T, topo):
     E("s", "dma_start", out=A("wI"), in_=ext("w"))
     E("y", "dma_start", out=A("kI"), in_=ext("kap"))
     E("y", "dma_start", out=A("tI"), in_=ext("th"))
-    E("y", "dma_start", out=A("vv"), in_=ext("val"))
     E("g", "iota", out=A("pI"), pattern=[[0, 1]], base=0, channel_multiplier=1)
     E("g", "iota", out=A("mI"), pattern=[[1, 128]], base=0, channel_multiplier=0)
     E("g", "iota", out=A("dI"), pattern=[[-1, 128]], base=0, channel_multiplier=1)
@@ -289,23 +287,27 @@ def rank_program(g, core, T, topo):
     settle("g", toks)
     sub = lambda a, b: T.W[:, rank * C + a:rank * C + b]
     e8 = topo.engines(core, T.cores[near[0]])
-    loc = [e for e in topo.engines(core, two) if e not in e8]
-    g.remote_dma_fused([RemoteDMATransfer(dst_ids=[dst(topo, k, core)], dma_engine_mask=bits(loc[2 * j:2 * j + 2]), remote_sem=T.sem.hin,
-                                          srcs=[sub(256 * j, 256 * j + 256)], dsts=[T.hb[:, 0:256]]) for j, k in enumerate(car)],
+    loc = [e for e in topo.engines(core, car[0]) if e not in e8]
+    parts = [(k, j, loc[2 * j:2 * j + 2]) for j, k in enumerate(car)] + [(k, j + 1, e8[2 * j:2 * j + 2]) for j, k in enumerate(plain)]
+    g.remote_dma_fused([RemoteDMATransfer(dst_ids=[dst(topo, k, core)], dma_engine_mask=bits(es), remote_sem=T.sem.hin,
+                                          srcs=[sub(256 * j, 256 * j + 256)], dsts=[T.hb[:]]) for k, j, es in parts],
                        local_sem=T.sem.lsA)
-    g.remote_dma_fused([RemoteDMATransfer(dst_ids=[dst(topo, two, core)], dma_engine_mask=bits(loc), remote_sem=T.sem.hin,
-                                          srcs=[sub(512, 1024)], dsts=[T.hp[:, 0:512]]),
-                        RemoteDMATransfer(dst_ids=[dst(topo, T.cores[q], core) for q in near], dma_engine_mask=bits(e8), remote_sem=T.sem.ag,
-                                          srcs=[sub(0, 512)], dsts=[sub(0, 512) for q in near])], local_sem=T.sem.lsA)
-    nown = 2 * len(car) + len(loc) + len(e8)
+    g.remote_dma_fused([RemoteDMATransfer(dst_ids=[dst(topo, T.cores[q], core) for q in near], dma_engine_mask=bits(e8),
+                                          remote_sem=T.sem.ag, srcs=[sub(0, 256)], dsts=[sub(0, 256) for q in near])],
+                       local_sem=T.sem.lsA)
+    nown = 2 * len(parts) + len(e8)
     note("rem", own, False, ("lsA", nown, {}))
-    nag = len(e8) * (2 * len(near) + 4 * len(far))
+    nag = len(e8) * 4 * (NR - 1)
     for q in range(NR):
         if q != rank:
             note("rem", A("W", c(q * C, q * C + C)), True, ("ag", nag, {}))
     small = {"channel_multiplier": 0, "allow_small_or_imprecise_dtypes": True}
     E("g", "iota", out=A("RS"), pattern=[[0, 8], [32767, 16]], base=0, **small)
-    E("g", "iota", out=A("s0I"), pattern=[[16, 8], [0, 128]], base=0, channel_multiplier=-1)
+    settle("y", [("qg", cnt["qg"], {})])
+    E("y", "dma_start", out=A("vv"), in_=ext("val"))
+    E("g", "iota", out=A("on1"), pattern=[[0, 1024]], base=1, **small)
+    E("g", "affine_select", out=A("Sel0"), in_=A("on1"), pattern=[[-16, 8], [0, 128]], compare_op=O.is_equal, fill=0.0, base=0,
+      channel_multiplier=1)
     E("g", "iota", out=A("TK"), pattern=[[0, 8], [-1, 16]], base=15, **small)
     E("g", "iota", out=A("r1"), pattern=[[0, 128], [256, 16]], base=-128, **small)
     E("g", "iota", out=A("r2"), pattern=[[0, 128], [-256, 16]], base=128, **small)
@@ -313,6 +315,7 @@ def rank_program(g, core, T, topo):
     cI = lambda k: A("ci1", c(k, k + 1))
     ts(A("I32"), A("dI"), 0, O.is_equal)
     ts(A("Ib"), A("dI"), 0, O.is_equal)
+    cp(A("hl"), A("mI"))
     ts(cI(0), A("pI"), 4, O.arith_shift_right)
     ts(cI(1), A("pI"), 15, O.bitwise_and)
     ts(cI(2), A("pI"), 1, O.bitwise_and)
@@ -331,17 +334,33 @@ def rank_program(g, core, T, topo):
     tr(A("p5", c(0, 128)), A("f1"))
     tr(A("p6", c(0, 128)), A("f2"))
     act(A("I8k"), A("Ib"), scale=8192.0)
+    act(A("I16k"), A("Ib"), scale=16384.0)
     act(A("nI"), A("Ib"), scale=-1.0)
+    act(A("hr"), ind(A("h0"), A("hl")))
     act(A("nm"), A("p5", c(0, 128)))
     act(A("pri"), A("p6", c(0, 128)))
     cp(K_("wf"), A("wI"))
     ts(A("Wb"), A("B"), K_("wf"), O.mult)
-    for s in range(3, 16):
+    for s in range(3, 9):
+        act(blk("Sel", s), A("B"), scale=A("oh16", c(s, s + 1)))
+    for s in range(9, 16):
         ts(blk("Sel", s), A("B"), A("oh16", c(s, s + 1)), O.mult)
     ts(K_("k16"), A("kI"), 16.0, O.mult)
     ts(K_("ev8"), K_("odd"), -8.0, O.mult, 8.0, O.add)
     ts(A("oddI"), A("Ib"), K_("odd"), O.mult)
     ts(A("ib"), A("mI"), -128.0, O.add)
+
+    def twin_sums(b):
+        for k in range(4 * b, 4 * b + 4):
+            mm(blk("pn", k), A("Ib"), A("tri"), k == 4 * b, False)
+            mm(blk("pn", k), blk("Sel0", k), A("nh"), False, False)
+            mm(blk("pn", k), blk("Sel0", k), A("nl"), False, k == 4 * b + 3)
+
+    def twin_flags(b):
+        for k in range(4 * b, 4 * b + 4):
+            act(blk("dab", k), blk("pn", k), F.Abs, bias=A("nn", c(k, k + 1)))
+        half = c(512 * b, 512 * b + 512)
+        act(A("eq", half), A("dab", half), F.Relu, scale=-1.0, bias=1.0)
 
     def prepare(t, h):
         L = slots(t)
@@ -349,34 +368,36 @@ def rank_program(g, core, T, topo):
         act(A("fr"), A("pri"), F.Sign, scale=-1.0, bias=32.5)
         group(A("p7", c(0, 128)), [(A("nm"), A("I32")), (A("Ib"), A("t8k")), (A("fr"), A("I8k"))])
         act(A("qh"), A("p7", c(0, 128)))
+        if t == 0:
+            for s in range(3, 16):
+                act(blk("KZ", s), A("Ib"), scale=float(VB + 128 * (POS[s] + 1)))
+        cp(A("i1"), A("p6", c(384, 512)))
         scan(A("M0"), A("RS"), A("pri"), O.min, O.max, 0.0)
+        ts(A("i2"), A("i1"), 4095, O.bitwise_and)
         tt(A("eq0"), spread("M0"), A("pri"), O.is_equal)
+        ts(A("i3"), A("i2"), K_("k16"), O.add)
+        group(A("pk", c(128, 256)), [(A("I32"), A("nm")), (A("I16k"), A("eq0"))])
         tt(A("ql"), A("p7", c(0, 128)), A("qh"), O.subtract)
         group(A("p6", c(0, 128)), [(A("oddI"), A("qh")), (A("oddI"), A("ql"))])
-        for j, s in enumerate(L):
-            group(blk("pn", j), [(blk("Sel", s), A("qh")), (blk("Sel", s), A("ql"))])
-        tt(A("PN"), A("eq0"), A("nm"), O.mult)
-        ts(A("sI"), spread("M0"), -1.0, O.mult, 1024.0, O.add)
-        scan(A("N0"), A("RS"), A("PN"), O.min, O.max, 0.0)
-        ts(A("sI"), A("sI"), 15, O.bitwise_and)
-        act(A("n0c"), spread("N0"))
+        tt(A("i4"), A("i2"), A("i3"), O.mult)
+        scan(A("N0"), A("RS"), A("pk", c(128, 256)), O.min, O.max, 0.0)
+        act(A("n0c"), spread("N0"), bias=-16384.0)
         tr(A("p7", c(256, 384)), A("n0c"))
         act(A("nh"), A("p7", c(256, 384)))
-        group(A("p7", c(256, 384)), [(A("n0c"), A("I32")), (A("nI"), A("nh"))])
+        for j, s in enumerate(L):
+            group(blk("pn", j), [(blk("Sel", s), A("qh")), (blk("Sel", s), A("ql"))])
+        ts(A("i5"), A("i4"), 4, O.arith_shift_right)
         act(A("An"), spread("N0"), bias=K_("nbc"))
-        act(A("nl"), A("p7", c(256, 384)))
-        act(A("nn"), A("N0", c(15, 128, 16)), scale=-1.0)
+        act(A("nn"), A("N0", c(15, 128, 16)), scale=-1.0, bias=16384.0)
         act(A("e1k"), A("eq0"), scale=1024.0)
         act(A("x1"), spread("M0"), F.Relu, scale=-2048.0, bias=2048.0 * 33)
         act(A("x2"), spread("M0"), F.Relu, scale=2048.0, bias=-2048.0 * (1024 - 32 * (t + 1)))
-        act(A("hr"), ind(A(h), A("hl")))
-        tt(A("sd"), A("sI"), A("dl"), O.mult)
-        group(A("pk", c(480, 488)), [(A("sd"), A("dc128")), (A("Ib"), A("Cl"))])
-        cp(A("i1"), A("p6", c(384, 512)))
-        ts(A("i2"), A("i1"), 4095, O.bitwise_and)
-        ts(A("i3"), A("i2"), K_("k16"), O.add)
-        tt(A("i4"), A("i2"), A("i3"), O.mult)
-        ts(A("i5"), A("i4"), 4, O.arith_shift_right)
+        if t:
+            act(A("hr"), ind(A(h), A("hl")))
+        else:
+            for s in range(16):
+                act(vslot(s), A("vv", c(s, None, 16)))
+        ts(A("sI"), spread("M0"), -1.0, O.mult, 1024.0, O.add)
         if t:
             ts(A("i6"), A("i5"), K_("odd"), O.mult, A("Ac", c(1, 2)), O.add)
             ts(A("i1"), A("i5"), A("Ac", c(0, 1)), O.add)
@@ -384,26 +405,25 @@ def rank_program(g, core, T, topo):
         else:
             ts(A("i6"), A("i5"), K_("odd"), O.mult, K_("ev8"), O.add)
             z = "i5"
+        ts(A("sI"), A("sI"), 15, O.bitwise_and)
         ts(A("i3"), A("i6"), 3, O.arith_shift_right, 1, O.bitwise_and)
+        tt(A("sd"), A("sI"), A("dl"), O.mult)
+        group(A("pk", c(480, 488)), [(A("sd"), A("dc128")), (A("Ib"), A("Cl"))])
         tt(A("i4"), A(z), A("i3"), O.mult)
         tt(A("i6"), A("i4"), A("p6", c(0, 128)), O.add)
         ts(A("aI"), A("i6"), 8191, O.bitwise_and)
         for j in range(len(L)):
             tt(blk("hit", j), A("aI"), blk("pn", j), O.is_equal)
+        tt(A("nl"), A("p7", c(256, 384)), A("nh"), O.subtract)
         group(A("p5", c(0, 128)), [(A("Ib"), A("ib"))] + [(blk("KZ", s), blk("hit", j)) for j, s in enumerate(L)])
         tt(A("off"), A("aI"), A("p5", c(0, 128)), O.max)
         cp(A("lst"), A("off"))
         tr(A("p6", c(128, 256)), A("off"))
-        for b in range(2):
-            mm(A("pn", c(512 * b, 512 * b + 512)), A("Ib"), A("tri"), True, False)
-            for k in range(4 * b, 4 * b + 4):
-                mm(blk("pn", k), blk("Sel0", k), A("nh"), False, False)
-                mm(blk("pn", k), blk("Sel0", k), A("nl"), False, k == 4 * b + 3)
-        for k in range(8):
-            act(blk("dab", k), blk("pn", k), F.Abs, bias=A("nn", c(k, k + 1)))
-        for b in range(2):
-            half = c(512 * b, 512 * b + 512)
-            act(A("eq", half), A("dab", half), F.Relu, scale=-1.0, bias=1.0)
+        twin_sums(0)
+        if t:
+            twin_sums(1)
+            twin_flags(0)
+            twin_flags(1)
 
     def reads(t, h):
         win = A("W", c(0, VD))
@@ -418,6 +438,8 @@ def rank_program(g, core, T, topo):
             out = A("pn", c(1024 + 16 * (a - TA), 1024 + 16 * (b - TA)))
             mm(out, A("nI"), A("hr", c(16 * a, 16 * b)), True, False)
             mm(out, A("Ib"), A("d", c(16 * a, 16 * b)), False, True)
+        if t == 0:
+            twin_sums(1)
         for a, b in ((0, A2), (A2, TA)):
             act(A("ad", c(16 * a, 16 * b)), A("d", c(16 * a, 16 * b)), F.Abs)
         act(A("ad", c(16 * TA, 2048)), A("pn", c(1024, 1024 + 16 * NB)), F.Abs)
@@ -425,47 +447,54 @@ def rank_program(g, core, T, topo):
         mm(key, A("Ib"), A("TK"), True, False)
         for k in range(16):
             mm(A("pk", c(k, 128, 16)), A("ad", c(k, None, 16)), A("B16"), False, k == 15)
+        if t == 0:
+            twin_flags(0)
+            twin_flags(1)
         scan(A("sh"), A("r1"), A("d"), O.min, O.max, -128.0)
         scan(A("sl"), A("r2"), A("d"), O.max, O.min, 128.0)
         hi, lo = A("sh", c(15, None, 16)), A("sl", c(15, None, 16))
+        scan(A("ME"), A("RS"), key, O.min, O.max, 0.0)
         group(A("p5", c(128, 256)), [(A("nI"), A("x1")), (A("Ib"), A("x2")), (hi, A("B")), (lo, A("nB"))])
         group(A("p5", c(0, 128)), [(hi, A("B")), (lo, A("nB"))])
-        mm(A("pn", c(0, 128)), A("Ib"), A("mh"), True, False)
-        mm(A("pn", c(0, TA)), A("I2"), A(h, c(0, TA)), False, False)
-        mm(A("pn", c(0, 128)), A("Ib"), hi, False, False)
-        mm(A("pn", c(0, 128)), A("Ib"), lo, False, True)
-        act(A("y1"), A("pn", c(0, 128)), scale=0.5, bias=MAGIC)
+        mm(A("pn", c(1536, 1664)), A("Ib"), A("mh"), True, False)
+        mm(A("pn", c(1536, 1536 + TA)), A("I2"), A(h, c(0, TA)), False, False)
+        mm(A("pn", c(1536, 1664)), A("Ib"), hi, False, False)
+        mm(A("pn", c(1536, 1664)), A("Ib"), lo, False, True)
+        tt(A("oh"), key, A("ME"), O.is_equal)
+        if t:
+            act(A("no"), A("oh"), scale=-1.0, bias=1.0)
+        else:
+            tt(A("no"), key, A("ME"), O.not_equal)
+        act(A("y1"), A("pn", c(1536, 1664)), scale=0.5, bias=MAGIC)
         act(A("yb"), A("y1"), bias=-MAGIC)
         tt(A("go"), A("p5", c(128, 256)), A("thE"), O.is_ge)
-        tt(A("Fd"), A("p5", c(0, 128)), A("th2"), O.is_ge)
         mm(A("p7", c(0, 128)), A("Ib"), A("ofd"), True, False)
         for k in range(8):
             mm(A("p7", c(16 * k, 16 * k + 16)), blk("eq", k), A("go", c(16 * k, 16 * k + 16)), False, k == 7)
-        scan(A("ME"), A("RS"), key, O.min, O.max, 0.0)
-        tt(A("oh"), key, A("ME"), O.is_equal)
-        tt(A("no"), key, A("ME"), O.not_equal)
         tt(A("PS"), A("oh"), A("p6", c(128, 256)), O.mult)
+        tt(A("Fd"), A("p5", c(0, 128)), A("th2"), O.is_ge)
         scan(A("SE"), A("no"), A("PS"), O.mult, O.add, 0.0)
-        ts(A("tg"), spread("SE"), -float(VB), O.add, A("cT", c(t, t + 1)), O.max)
-        tt(A("l1"), A("tg"), A("dl"), O.mult)
-        group(A("pn", c(512, 520)), [(A("Fd"), A("rh2")), (A("l1"), A("dc"))])
         tt(A("l2"), A("go"), A("p7", c(0, 128)), O.is_gt)
-        cp(A("sl16"), A("pn", c(512, 520)))
+        ts(A("tg"), spread("SE"), -float(VB), O.add, A("cT", c(t, t + 1)), O.max)
         tt(A("l2"), A("l2"), A("An"), O.mult)
+        tt(A("l1"), A("tg"), A("dl"), O.mult)
         group(A("pn", c(1024, 1032)), [(A("I32"), A("Cd")), (A("l2"), A("dc"))])
-        E("v", "tensor_copy", out=ind(A("W", c(VB, WEND)), A("sl16")), in_=A("yb"))
         act(A("rv", t, rank, c(128, 136)), A("pn", c(1024, 1032)))
-        E("v", "tensor_copy", out=A("rv", t, rank, c(0, 128)), in_=ind(A("W", c(VB, WEND)), A("vl")))
+        group(A("pn", c(512, 520)), [(A("Fd"), A("rh2")), (A("l1"), A("dc"))])
+        cp(A("sl16"), A("pn", c(512, 520)))
+        E("v", "tensor_copy", out=ind(A("W", c(VB, WEND)), A("sl16")), in_=A("yb"))
         tt(A("rv", t, rank, c(136, 144)), A("pn", c(1024, 1032)), A("rv", t, rank, c(128, 136)), O.subtract)
+        E("v", "tensor_copy", out=A("rv", t, rank, c(0, 128)), in_=ind(A("W", c(VB, VD)), A("vl")))
         toks = []
         need("g", A("rv", t, rank), False, toks)
         settle("g", toks)
         piece = T.rv[:, t, rank, :]
-        sends = [RemoteDMATransfer(dst_ids=[dst(topo, k, core)], dma_engine_mask=bits(loc[4 * j:4 * j + 4]), remote_sem=T.sem["rl%d" % t],
-                                   srcs=[piece], dsts=[piece]) for j, (k, _) in enumerate(relay)]
-        sends.append(RemoteDMATransfer(dst_ids=[dst(topo, T.cores[q], core) for q in near], dma_engine_mask=bits(e8),
-                                       remote_sem=T.sem["dr%d" % t], srcs=[piece], dsts=[piece for q in near]))
-        g.remote_dma_fused(sends, local_sem=T.sem.lsD)
+        g.remote_dma_fused([RemoteDMATransfer(dst_ids=[dst(topo, k, core)], dma_engine_mask=bits(es), remote_sem=T.sem["rl%d" % t],
+                                              srcs=[piece], dsts=[piece]) for (k, _), es in zip(relay, (loc[:4], e8[:4], loc[4:], e8[4:]))],
+                           local_sem=T.sem.lsD)
+        g.remote_dma_fused([RemoteDMATransfer(dst_ids=[dst(topo, T.cores[q], core) for q in near], dma_engine_mask=bits(e8),
+                                              remote_sem=T.sem["dr%d" % t], srcs=[piece], dsts=[piece for q in near])],
+                           local_sem=T.sem.lsD)
         for q in range(NR):
             if q != rank:
                 note("rem", A("rv", t, q), True, ("dr%d" % t, len(e8) * (NR - 1), {}))
@@ -473,32 +502,31 @@ def rank_program(g, core, T, topo):
     def update(t, h, hn):
         group(A("pn", c(0, 128)), [(A("Ib"), A("yb")), (A("nI"), A(h))])
         act(A(hn), A("pn", c(0, 128)), F.Abs)
-        mm(A("pn", c(1536, 1544)), A("yb"), A("B1"), True, True)
+        group(A("pn", c(1536, 1544)), [(A("yb"), A("B8th")), (A("Ib"), A("c716"))])
+        act(A("r8", c(0, 8)), A("pn", c(1536, 1544)), bias=MAGIC)
+        act(A("r8", c(8, 16)), A("r8", c(0, 8)), scale=256.0, bias=-256.0 * MAGIC)
+        group(A("pn", c(1024, 1032)), [(A("yb"), A("Bm32")), (A("Ib"), A("c960", c(8 * t, 8 * t + 8))), (A("I32"), A("r8", c(8, 16)))])
         if t < STEPS - 1:
+            ac = lambda k: A("Ac", c(k, k + 1))
             mm(A("pn", c(512, 640)), A("on32"), A("Fd"), True, True)
-            act(A("f1"), A("pn", c(512, 640)), accum_out=A("Ac", c(2, 3)))
+            act(A("f1"), A("pn", c(512, 640)), scale=1.0 / 64, bias=-63.0 / 16384, accum_out=ac(2))
+            act(ac(3), ac(2), bias=MAGIC)
+            act(ac(4), ac(2), scale=64.0, bias=31.5)
+            act(ac(5), ac(3), scale=-64.0, bias=64.0 * MAGIC)
+            act(ac(0), ac(5), bias=ac(4))
+            act(ac(1), ac(0), scale=K_("odd"), bias=K_("ev8"))
         s = lambda k: A("sm", c(8 * k, 8 * k + 8))
-        si = lambda k: A("smi", c(8 * k, 8 * k + 8))
         col = lambda n, k: A(n, c(k, 128, 16))
         tt(A("f2"), A("go"), A("e1k"), O.mult)
         ts(s(0), col("SE", 15), float(VB), O.is_lt)
         tt(s(1), col("p5", 15), col("thE", 15), O.is_lt)
-        cp(si(0), A("pn", c(1536, 1544)))
         tt(s(3), col("SE", 15), col("nm", t), O.subtract)
         tt(s(2), s(0), s(1), O.mult)
-        ts(si(1), si(0), 7, O.bitwise_and)
-        tt(s(3), s(3), s(2), O.mult)
-        ts(s(4), si(1), -32.0, O.mult, 960.0 - 32 * t, O.add)
-        tt(col("nm", t), col("nm", t), s(3), O.add)
-        tt(s(4), s(4), s(2), O.mult)
         tt(A("pri"), A("pri"), A("f2"), O.subtract)
+        tt(s(3), s(3), s(2), O.mult)
+        tt(s(4), A("pn", c(1024, 1032)), s(2), O.mult)
+        tt(col("nm", t), col("nm", t), s(3), O.add)
         tt(col("pri", t), col("pri", t), s(4), O.add)
-        if t < STEPS - 1:
-            ai = lambda k: A("smi", c(16 + k, 17 + k))
-            cp(ai(0), A("Ac", c(2, 3)))
-            ts(ai(1), ai(0), 63, O.bitwise_and)
-            cp(A("Ac", c(0, 1)), ai(1))
-            ts(A("Ac", c(1, 2)), ai(1), K_("odd"), O.mult, K_("ev8"), O.add)
 
     def drains(t):
         tt(A("dcd"), A("rv", t, c(None), c(128, 136)), A("rv", t, c(None), c(136, 144)), O.add)
@@ -506,45 +534,37 @@ def rank_program(g, core, T, topo):
         for q in range(NR - 1, -1, -1):
             E("v", "tensor_copy", out=ind(A("W", c(0, VB)), A("dL", c(8 * q, 8 * q + 8))), in_=A("rv", t, q, c(0, 128)))
 
-    for s in range(3, 16):
-        act(blk("KZ", s), A("Ib"), scale=float(VB + 128 * (POS[s] + 1)))
+    fill(A("on32"), 1.0)
+    cp(K_("tf"), A("tI"))
+    ts(A("thd"), A("I32"), K_("tf"), O.mult)
+    mm(A("p5", c(256, 384)), A("on32"), A("thd"), True, True)
     ts(A("xl"), A("mI", c(0, 8)), 16.0, O.mult, 15.0, O.add)
-    cp(A("hl"), A("mI"))
     ts(A("mm"), A("mI"), 15, O.bitwise_and)
     ts(A("dl"), A("mm"), K_("pmf"), O.is_equal)
     ts(A("dc"), A("mI", c(0, 8)), K_("pdf"), O.is_equal)
     ts(A("dc128"), A("dc"), 128.0, O.mult)
     ts(A("Cl"), A("mI", c(0, 8)), 16.0, O.mult, K_("pmf"), O.add)
-    ts(K_("nbc"), K_("pf"), -1.0, O.mult, -float(DUMP), O.add)
-    for k in range(4):
-        ts(blk("tri", k), A("dI"), 0, O.is_ge, 16384.0, O.mult)
-    ts(A("Sel0"), A("s0I"), 0, O.is_equal)
-    prepare(0, H[0])
+    ts(K_("nbc"), K_("pf"), -1.0, O.mult, -16384.0 - DUMP, O.add)
+    ts(A("tri"), A("dI"), 0, O.is_ge, 16384.0, O.mult)
     for k in range(3):
         ts(A("cT", c(k, k + 1)), K_("pf"), 128.0 * POS[k], O.add)
     ts(A("ofd"), A("mm"), K_("pmf"), O.not_equal, 4.0, O.mult)
-    ts(A("B1"), A("dc"), 1.0, O.mult)
+    ts(A("B8th"), A("dc"), 0.125, O.mult)
+    ts(A("Bm32"), A("dc"), -32.0, O.mult)
+    fill(A("c716"), -0.4375)
+    for k in range(STEPS):
+        fill(A("c960", c(8 * k, 8 * k + 8)), 960.0 - 32 * k)
     ts(A("B16"), A("dc"), 16.0, O.mult)
     ts(A("Cd"), A("Cl"), float(DUMP), O.add)
     ts(A("rh2"), A("dc"), 2048.0, O.mult)
     fill(A("W", c(DUMP, VB)), 0.0)
-    fill(A("W", c(VD, WEND)), 0.0)
-    fill(A("on32"), 1.0)
     fill(A("mh"), -0.5)
-    cp(K_("tf"), A("tI"))
-    ts(A("thd"), A("I32"), K_("tf"), O.mult)
-    mm(A("p5", c(256, 384)), A("on32"), A("thd"), True, True)
-    vslot = lambda s: A("W", c(VB + 128 * POS[s], VB + 128 * POS[s] + 128))
-    for s in range(16):
-        if s % 2:
-            act(vslot(s), A("vv", c(s, None, 16)))
-        else:
-            cp(vslot(s), A("vv", c(s, None, 16)))
+    ts(A("th2"), A("ofd"), 1024.0, O.mult)
     act(A("thE"), A("p5", c(256, 384)))
-    ts(A("f1"), A("ofd"), 1024.0, O.mult)
-    tt(A("th2"), A("thE"), A("f1"), O.add)
     act(A("nB"), A("B"), scale=-1.0)
     act(A("I2"), A("Ib"), scale=2.0)
+    prepare(0, H[0])
+    tt(A("th2"), A("thE"), A("th2"), O.add)
     for t in range(STEPS):
         h, hn = H[t % 2], H[1 - t % 2]
         reads(t, h)
@@ -570,7 +590,7 @@ def rank_program(g, core, T, topo):
             E("y", "dma_start", out=ext("yval"), in_=A("vv"))
         drains(t)
     E("y", "dma_start", out=ext("ymem"), in_=A("W", c(rank * C, rank * C + C)))
-    g.wait_ge(T.sem.lsD, STEPS * (8 + len(e8)))
+    g.wait_ge(T.sem.lsD, STEPS * (2 * len(e8) + len(loc)))
     for k in range(ndma[0]):
         if not any(seen[q].get("dm%d" % k, 0) for q in Q):
             g.sync.wait_ge(T.sem["dm%d" % k], 16)

from concourse.mybir import dt, AluOpType as O, AxisListType, ActivationFunctionType as F
from concourse.bass import DstId, RemoteDMATransfer

NR, C, TH, STEPS = 8, 1024, 128, 3
DUMP = NR * C
VB = DUMP + TH
VD = VB + 16 * TH
WEND = VD + 16 * TH
PW = 144
MAGIC = 12582912.0
POS = [2, 1, 0] + list(range(3, 16))
NB = 48
TA = TH - NB

S, P = "sbuf", "psum"
SCRATCH = {
    "W": (S, [128, WEND], "bfloat16"), "vv": (S, [128, 16 * TH], "bfloat16"),
    "hb": (S, [128, 256], "bfloat16"),
    "pI": (S, [128, 1], "int32"), "mI": (S, [128, 128], "int32"), "dI": (S, [128, 128], "int32"),
    "ci1": (S, [128, 4], "int32"), "cols": (S, [128, 16], "float32"), "cT": (S, [128, 3], "float32"),
    "md": (S, [128, 128], "int32"), "mm": (S, [128, 128], "int32"),
    "I32": (S, [128, 128], "float32"), "Ib": (S, [128, 128], "bfloat16"), "nI": (S, [128, 128], "bfloat16"),
    "I2": (S, [128, 128], "bfloat16"), "oddI": (S, [128, 128], "bfloat16"), "I8k": (S, [128, 128], "bfloat16"),
    "I16k": (S, [128, 128], "bfloat16"),
    "B": (S, [128, 128], "bfloat16"), "nB": (S, [128, 128], "bfloat16"), "dl": (S, [128, 128], "bfloat16"),
    "ofd": (S, [128, 128], "bfloat16"), "dc": (S, [128, 8], "float32"), "B8th": (S, [128, 8], "bfloat16"),
    "Bm32": (S, [128, 8], "bfloat16"), "c716": (S, [128, 8], "bfloat16"), "c960": (S, [128, 24], "bfloat16"),
    "B16": (S, [128, 8], "bfloat16"), "dc128": (S, [128, 8], "bfloat16"), "Cl": (S, [128, 8], "bfloat16"),
    "Cd": (S, [128, 8], "float32"), "rh2": (S, [128, 8], "float32"), "oh16": (S, [128, 16], "float32"),
    "Sel": (S, [128, 2048], "bfloat16"), "KZ": (S, [128, 2048], "bfloat16"),
    "TK": (S, [128, 128], "bfloat16"), "RS": (S, [128, 128], "float32"),
    "xl": (S, [128, 8], "uint16"), "hl": (S, [128, 128], "uint16"),
    "r1": (S, [128, 2048], "bfloat16"), "r2": (S, [128, 2048], "bfloat16"),
    "tri": (S, [128, 128], "bfloat16"), "on1": (S, [128, 1024], "bfloat16"), "Sel0": (S, [128, 1024], "bfloat16"),
    "nn": (S, [128, 8], "float32"), "on32": (S, [128, 128], "float32"), "t8k": (S, [128, 128], "bfloat16"),
    "mh": (S, [128, 128], "bfloat16"), "ib": (S, [128, 128], "bfloat16"),
    "wI": (S, [128, 1], "int32"), "kI": (S, [128, 1], "int32"), "tI": (S, [128, 1], "int32"),
    "Wb": (S, [128, 128], "bfloat16"), "thd": (S, [128, 128], "float32"), "thE": (S, [128, 128], "float32"),
    "th2": (S, [128, 128], "float32"),
    "L1": (S, [128, 128], "int32"), "L2": (S, [128, 128], "int32"), "f1": (S, [128, 128], "float32"),
    "f2": (S, [128, 128], "float32"),
    "h0": (S, [128, 128], "bfloat16"), "h1": (S, [128, 128], "bfloat16"),
    "nm": (S, [128, 128], "float32"), "pri": (S, [128, 128], "float32"),
    "fr": (S, [128, 128], "bfloat16"), "qh": (S, [128, 128], "bfloat16"), "ql": (S, [128, 128], "bfloat16"),
    "i1": (S, [128, 128], "int32"), "i2": (S, [128, 128], "int32"), "i3": (S, [128, 128], "int32"),
    "i4": (S, [128, 128], "int32"), "i5": (S, [128, 128], "int32"), "i6": (S, [128, 128], "int32"),
    "aI": (S, [128, 128], "int32"), "hit": (S, [128, 2048], "bfloat16"), "off": (S, [128, 128], "float32"),
    "lst": (S, [128, 128], "uint16"), "hr": (S, [128, 2048], "bfloat16"), "d": (S, [128, 2048], "bfloat16"),
    "ad": (S, [128, 2048], "bfloat16"), "sh": (S, [128, 2048], "bfloat16"), "sl": (S, [128, 2048], "bfloat16"),
    "M0": (S, [128, 128], "float32"), "eq0": (S, [128, 128], "bfloat16"), "e1k": (S, [128, 128], "bfloat16"),
    "N0": (S, [128, 128], "float32"), "n0c": (S, [128, 128], "float32"),
    "sI": (S, [128, 128], "int32"), "sd": (S, [128, 128], "bfloat16"), "vl": (S, [128, 8], "uint16"),
    "x1": (S, [128, 128], "bfloat16"), "x2": (S, [128, 128], "bfloat16"), "An": (S, [128, 128], "float32"),
    "nh": (S, [128, 128], "bfloat16"), "nl": (S, [128, 128], "bfloat16"), "dab": (S, [128, 1024], "bfloat16"),
    "eq": (S, [128, 1024], "bfloat16"), "y1": (S, [128, 128], "float32"), "yb": (S, [128, 128], "bfloat16"),
    "ME": (S, [128, 128], "float32"), "oh": (S, [128, 128], "float32"), "no": (S, [128, 128], "float32"),
    "PS": (S, [128, 128], "float32"), "SE": (S, [128, 128], "float32"), "go": (S, [128, 128], "bfloat16"),
    "Fd": (S, [128, 128], "float32"), "r8": (S, [128, 16], "float32"),
    "tg": (S, [128, 128], "float32"), "l1": (S, [128, 128], "float32"), "l2": (S, [128, 128], "float32"),
    "sl16": (S, [128, 8], "uint16"), "sm": (S, [128, 64], "float32"),
    "Ac": (S, [128, 8], "float32"), "rv": (S, [128, STEPS, NR, PW], "bfloat16"), "dcd": (S, [128, 64], "float32"),
    "dL": (S, [128, 64], "uint16"),
    "pn": (P, [128, 2048], "float32"), "pk": (P, [128, 512], "float32"), "p5": (P, [128, 512], "float32"),
    "p6": (P, [128, 512], "float32"), "p7": (P, [128, 512], "float32"),
}
SEMAPHORES = ["qg", "qv", "qs", "qt", "ag", "lsA", "lsD", "hin", "hout"] + ["dr%d" % t for t in range(STEPS)] \
    + ["rl%d" % t for t in range(STEPS)] + ["dm%d" % k for k in range(16)]


def dst(topo, d, src):
    rid, pid = topo.addr(d, src)
    return DstId(rid=rid, pnc=pid)


def bits(es):
    m = 0
    for e in es:
        m |= 1 << e
    return m


def roles(T, topo, r):
    me = T.cores[r]
    near = [q for q in range(NR) if q != r and topo.may_write(me, T.cores[q])]
    far = [q for q in range(NR) if q != r and q not in near]
    chip = [c for c in topo.cores_of(me) if c != me]
    car = [c for c in chip if topo.may_write(c, T.cores[far[0]])]
    car = sorted(car, key=lambda c: (topo.die(c) != topo.die(me), c))
    plain = [c for c in chip if c not in car]
    a = sum(q < r for q in near)
    relay = [(car[(a + b) % 2 * 2 + b // 2], q) for b, q in enumerate(far)]
    return near, far, car, plain, relay


def helper_program(g, core, T, topo):
    for r in range(NR):
        me = T.cores[r]
        if core not in topo.cores_of(me):
            continue
        near, far, car, plain, relay = roles(T, topo, r)
        n = 0
        if core in car or core in plain:
            serve = far if core in car else near
            lo = r * C + 256 * (car.index(core) if core in car else 1 + plain.index(core))
            es = topo.engines(core, T.cores[serve[0]])
            g.wait_ge(T.sem.hin, 2)
            g.remote_dma_fused([RemoteDMATransfer(dst_ids=[dst(topo, T.cores[q], core) for q in serve], dma_engine_mask=bits(es),
                                                  remote_sem=T.sem.ag, srcs=[T.hb[:]],
                                                  dsts=[T.W[:, lo:lo + 256] for q in serve])], local_sem=T.sem.hout)
            n += len(es)
        for c, q in relay:
            if c != core:
                continue
            es = topo.engines(core, T.cores[q])
            for t in range(STEPS):
                g.wait_ge(T.sem["rl%d" % t], 4)
                g.remote_dma_fused([RemoteDMATransfer(dst_ids=[dst(topo, T.cores[q], core)], dma_engine_mask=bits(es),
                                                      remote_sem=T.sem["dr%d" % t], srcs=[T.rv[:, t, r, :]],
                                                      dsts=[T.rv[:, t, r, :]])], local_sem=T.sem.hout)
                n += len(es)
        if n:
            g.wait_ge(T.sem.hout, n)


def rank_program(g, core, T, topo):
    rank = T.rank_of(core)
    if rank is None:
        helper_program(g, core, T, topo)
        return
    near, far, car, plain, relay = roles(T, topo, rank)

    Q = {"g": g, "v": g.vector, "s": g.scalar, "t": g.tensor, "y": g.sync}
    cnt, seen, log, ndma = {}, {q: {} for q in Q}, {}, [0]

    def A(name, *idx):
        ap = T[name]
        shape = [int(x) for x in ap.shape][1:]
        idx = idx + (slice(None),) * (len(shape) - len(idx))
        lo = hi = 0
        for n, i in zip(shape, idx):
            if isinstance(i, slice):
                a, b, st = i.indices(n)
                last = a + (b - 1 - a) // st * st
            else:
                a = last = i
            lo, hi = lo * n + a, hi * n + last
        return {"ap": ap[(slice(None),) + idx], "n": name, "r": (lo, hi + 1), "ind": None}

    def ind(win, offs):
        return {"ap": win["ap"].indirect(offs["ap"]), "n": win["n"], "r": win["r"], "ind": offs}

    def spans(v):
        lo, hi = v["r"]
        if v["n"] in SCRATCH and SCRATCH[v["n"]][0] == P:
            return True, lo // 512 * 512, (hi + 511) // 512 * 512
        return False, lo, hi

    def need(q, v, write, acc):
        ps, lo, hi = spans(v)
        for e in log.get(v["n"], []):
            if e["lo"] < hi and lo < e["hi"]:
                same = e["q"] == q
                if same and (ps and q == "t" or not e["w"]):
                    continue
                if e["w"] or write or ps and not same:
                    acc.append(e["tok"])

    def note(q, v, write, tok):
        ps, lo, hi = spans(v)
        L = log.setdefault(v["n"], [])
        if write:
            L[:] = [e for e in L if not (lo <= e["lo"] and e["hi"] <= hi and not ps)]
        if ps:
            L[:] = [e for e in L if not (e["q"] == q and e["w"] == write and e["lo"] == lo and e["hi"] == hi)]
        L.append({"lo": lo, "hi": hi, "w": write, "q": q, "tok": tok})

    def settle(q, toks):
        best = {}
        for s, n, snap in toks:
            if seen[q].get(s, 0) < n and best.get(s, (0, 0))[0] < n:
                best[s] = (n, snap)
        for s in list(best):
            if any(o != s and best[o][1].get(s, 0) >= best[s][0] for o in best):
                del best[s]
        for s in best:
            n, snap = best[s]
            Q[q].wait_ge(T.sem[s], n)
            for k in snap:
                seen[q][k] = max(seen[q].get(k, 0), snap[k])
            seen[q][s] = n

    calls = {"t": {"matmul": g.tensor.matmul, "transpose": g.tensor.transpose},
             "s": {"activation": g.scalar.activation, "dma_start": g.scalar.dma_start},
             "y": {"dma_start": g.sync.dma_start}, "g": {"iota": g.iota, "affine_select": g.affine_select},
             "v": {"tensor_copy": g.vector.tensor_copy, "tensor_tensor": g.vector.tensor_tensor, "memset": g.vector.memset,
                   "tensor_scalar": g.vector.tensor_scalar, "tensor_tensor_scan": g.vector.tensor_tensor_scan}}

    def E(q, meth, _pos=(), **kw):
        wr, rd = [], []
        for k, v in list(kw.items()) + [("ap", p) for p in _pos]:
            if isinstance(v, dict):
                (wr if k in ("out", "ap", "accum_out") else rd).append(v)
                if v["ind"]:
                    rd.append(v["ind"])
        toks = []
        for v in rd:
            need(q, v, False, toks)
        for v in wr:
            need(q, v, True, toks)
        settle(q, toks)
        un = lambda v: v["ap"] if isinstance(v, dict) else v
        ins = calls[q][meth](*[un(p) for p in _pos], **{k: un(v) for k, v in kw.items()})
        if meth == "dma_start":
            s, n = "dm%d" % ndma[0], 16
            ndma[0] += 1
            ins.then_inc(T.sem[s], 16)
        else:
            s = "q" + q
            cnt[s] = n = cnt.get(s, 0) + 1
            ins.then_inc(T.sem[s], 1)
        tok = (s, n, dict(seen[q]))
        dq = q if meth != "dma_start" else "dma"
        for v in rd:
            note(dq, v, False, tok)
        for v in wr:
            note(dq, v, True, tok)

    def cp(out, in_):
        E("v", "tensor_copy", out=out, in_=in_)

    def tt(out, a, b, op):
        E("v", "tensor_tensor", out=out, in0=a, in1=b, op=op)

    def ts(out, a, s1, op0, s2=None, op1=None):
        if op1 is None:
            E("v", "tensor_scalar", out=out, in0=a, scalar1=s1, scalar2=None, op0=op0)
        else:
            E("v", "tensor_scalar", out=out, in0=a, scalar1=s1, scalar2=s2, op0=op0, op1=op1)

    def act(out, in_, func=F.Identity, **kw):
        E("s", "activation", out=out, in_=in_, func=func, **kw)

    def mm(out, lhsT, rhs, start, stop):
        E("t", "matmul", out=out, lhsT=lhsT, rhs=rhs, start=start, stop=stop)

    def tr(out, in_):
        E("t", "transpose", out=out, in_=in_, identity=A("I32"))

    def group(out, pairs):
        for k, (a, b) in enumerate(pairs):
            mm(out, a, b, k == 0, k == len(pairs) - 1)

    def scan(out, d0, d1, op0, op1, init):
        E("v", "tensor_tensor_scan", out=out, data0=d0, data1=d1, initial=init, op0=op0, op1=op1)

    def fill(v, x):
        E("v", "memset", (v, x))

    def ext(name):
        return {"ap": T[name][:], "n": name, "r": (0, 1), "ind": None}

    c = slice
    COLS = ["pdf", "pmf", "pf", "odd", "ev8", "nbc", "key", "wf", "k16", "tf"]
    K_ = lambda n: A("cols", c(COLS.index(n), COLS.index(n) + 1))
    blk = lambda n, k: A(n, c(128 * k, 128 * k + 128))
    spread = lambda n: ind(A(n), A("xl"))
    vslot = lambda s: A("W", c(VB + 128 * POS[s], VB + 128 * POS[s] + 128))
    H = ["h0", "h1"]

    def slots(t):
        return [s for s in range(16) if s >= STEPS or s < t]

    E("y", "dma_start", out=A("W", c(rank * C, rank * C + C)), in_=ext("mem"))
    E("s", "dma_start", out=A("L1"), in_=ext("pnd"))
    E("s", "dma_start", out=A("L2"), in_=ext("due"))
    E("y", "dma_start", out=A("h0"), in_=ext("h"))
    E("s", "dma_start", out=A("wI"), in_=ext("w"))
    E("y", "dma_start", out=A("kI"), in_=ext("kap"))
    E("y", "dma_start", out=A("tI"), in_=ext("th"))
    E("g", "iota", out=A("pI"), pattern=[[0, 1]], base=0, channel_multiplier=1)
    E("g", "iota", out=A("mI"), pattern=[[1, 128]], base=0, channel_multiplier=0)
    E("g", "iota", out=A("dI"), pattern=[[-1, 128]], base=0, channel_multiplier=1)

    toks = []
    own = A("W", c(rank * C, rank * C + C))
    need("g", own, False, toks)
    settle("g", toks)
    sub = lambda a, b: T.W[:, rank * C + a:rank * C + b]
    e8 = topo.engines(core, T.cores[near[0]])
    loc = [e for e in topo.engines(core, car[0]) if e not in e8]
    parts = [(k, j, loc[2 * j:2 * j + 2]) for j, k in enumerate(car)] + [(k, j + 1, e8[2 * j:2 * j + 2]) for j, k in enumerate(plain)]
    g.remote_dma_fused([RemoteDMATransfer(dst_ids=[dst(topo, k, core)], dma_engine_mask=bits(es), remote_sem=T.sem.hin,
                                          srcs=[sub(256 * j, 256 * j + 256)], dsts=[T.hb[:]]) for k, j, es in parts],
                       local_sem=T.sem.lsA)
    g.remote_dma_fused([RemoteDMATransfer(dst_ids=[dst(topo, T.cores[q], core) for q in near], dma_engine_mask=bits(e8),
                                          remote_sem=T.sem.ag, srcs=[sub(0, 256)], dsts=[sub(0, 256) for q in near])],
                       local_sem=T.sem.lsA)
    nown = 2 * len(parts) + len(e8)
    note("rem", own, False, ("lsA", nown, {}))
    nag = len(e8) * 4 * (NR - 1)
    for q in range(NR):
        if q != rank:
            note("rem", A("W", c(q * C, q * C + C)), True, ("ag", nag, {}))
    small = {"channel_multiplier": 0, "allow_small_or_imprecise_dtypes": True}
    E("g", "iota", out=A("RS"), pattern=[[0, 8], [32767, 16]], base=0, **small)
    settle("y", [("qg", cnt["qg"], {})])
    E("y", "dma_start", out=A("vv"), in_=ext("val"))
    E("g", "iota", out=A("on1"), pattern=[[0, 1024]], base=1, **small)
    E("g", "affine_select", out=A("Sel0"), in_=A("on1"), pattern=[[-16, 8], [0, 128]], compare_op=O.is_equal, fill=0.0, base=0,
      channel_multiplier=1)
    E("g", "iota", out=A("TK"), pattern=[[0, 8], [-1, 16]], base=15, **small)
    E("g", "iota", out=A("r1"), pattern=[[0, 128], [256, 16]], base=-128, **small)
    E("g", "iota", out=A("r2"), pattern=[[0, 128], [-256, 16]], base=128, **small)

    cI = lambda k: A("ci1", c(k, k + 1))
    ts(A("I32"), A("dI"), 0, O.is_equal)
    ts(A("Ib"), A("dI"), 0, O.is_equal)
    cp(A("hl"), A("mI"))
    ts(cI(0), A("pI"), 4, O.arith_shift_right)
    ts(cI(1), A("pI"), 15, O.bitwise_and)
    ts(cI(2), A("pI"), 1, O.bitwise_and)
    ts(A("md"), A("mI"), 4, O.arith_shift_right)
    cp(K_("pdf"), cI(0))
    cp(K_("pmf"), cI(1))
    cp(K_("odd"), cI(2))
    cp(K_("pf"), A("pI"))
    ts(A("B"), A("md"), K_("pdf"), O.is_equal)
    ts(A("oh16"), A("mI", c(0, 16)), K_("pmf"), O.is_equal)
    ts(K_("key"), A("oh16", c(0, 1)), 14.0, O.mult, 1008.0, O.add)
    tt(K_("key"), K_("key"), K_("pmf"), O.subtract)
    fill(A("t8k"), 8192.0)
    cp(A("f1"), A("L1"))
    ts(A("f2"), A("L2"), -32.0, O.mult, K_("key"), O.add)
    tr(A("p5", c(0, 128)), A("f1"))
    tr(A("p6", c(0, 128)), A("f2"))
    act(A("I8k"), A("Ib"), scale=8192.0)
    act(A("I16k"), A("Ib"), scale=16384.0)
    act(A("nI"), A("Ib"), scale=-1.0)
    act(A("hr"), ind(A("h0"), A("hl")))
    act(A("nm"), A("p5", c(0, 128)))
    act(A("pri"), A("p6", c(0, 128)))
    cp(K_("wf"), A("wI"))
    ts(A("Wb"), A("B"), K_("wf"), O.mult)
    for s in range(3, 9):
        act(blk("Sel", s), A("B"), scale=A("oh16", c(s, s + 1)))
    for s in range(9, 16):
        ts(blk("Sel", s), A("B"), A("oh16", c(s, s + 1)), O.mult)
    ts(K_("k16"), A("kI"), 16.0, O.mult)
    ts(K_("ev8"), K_("odd"), -8.0, O.mult, 8.0, O.add)
    ts(A("oddI"), A("Ib"), K_("odd"), O.mult)
    ts(A("ib"), A("mI"), -128.0, O.add)

    def twin_sums(b):
        for k in range(4 * b, 4 * b + 4):
            mm(blk("pn", k), A("Ib"), A("tri"), k == 4 * b, False)
            mm(blk("pn", k), blk("Sel0", k), A("nh"), False, False)
            mm(blk("pn", k), blk("Sel0", k), A("nl"), False, k == 4 * b + 3)

    def twin_flags(b):
        for k in range(4 * b, 4 * b + 4):
            act(blk("dab", k), blk("pn", k), F.Abs, bias=A("nn", c(k, k + 1)))
        half = c(512 * b, 512 * b + 512)
        act(A("eq", half), A("dab", half), F.Relu, scale=-1.0, bias=1.0)

    def prepare(t, h):
        L = slots(t)
        mm(A("p6", c(384, 512)), A("Wb"), A(h), True, True)
        act(A("fr"), A("pri"), F.Sign, scale=-1.0, bias=32.5)
        group(A("p7", c(0, 128)), [(A("nm"), A("I32")), (A("Ib"), A("t8k")), (A("fr"), A("I8k"))])
        act(A("qh"), A("p7", c(0, 128)))
        if t == 0:
            for s in range(3, 16):
                act(blk("KZ", s), A("Ib"), scale=float(VB + 128 * (POS[s] + 1)))
        cp(A("i1"), A("p6", c(384, 512)))
        scan(A("M0"), A("RS"), A("pri"), O.min, O.max, 0.0)
        ts(A("i2"), A("i1"), 4095, O.bitwise_and)
        tt(A("eq0"), spread("M0"), A("pri"), O.is_equal)
        ts(A("i3"), A("i2"), K_("k16"), O.add)
        group(A("pk", c(128, 256)), [(A("I32"), A("nm")), (A("I16k"), A("eq0"))])
        tt(A("ql"), A("p7", c(0, 128)), A("qh"), O.subtract)
        group(A("p6", c(0, 128)), [(A("oddI"), A("qh")), (A("oddI"), A("ql"))])
        tt(A("i4"), A("i2"), A("i3"), O.mult)
        scan(A("N0"), A("RS"), A("pk", c(128, 256)), O.min, O.max, 0.0)
        act(A("n0c"), spread("N0"), bias=-16384.0)
        tr(A("p7", c(256, 384)), A("n0c"))
        act(A("nh"), A("p7", c(256, 384)))
        for j, s in enumerate(L):
            group(blk("pn", j), [(blk("Sel", s), A("qh")), (blk("Sel", s), A("ql"))])
        ts(A("i5"), A("i4"), 4, O.arith_shift_right)
        act(A("An"), spread("N0"), bias=K_("nbc"))
        act(A("nn"), A("N0", c(15, 128, 16)), scale=-1.0, bias=16384.0)
        act(A("e1k"), A("eq0"), scale=1024.0)
        act(A("x1"), spread("M0"), F.Relu, scale=-2048.0, bias=2048.0 * 33)
        act(A("x2"), spread("M0"), F.Relu, scale=2048.0, bias=-2048.0 * (1024 - 32 * (t + 1)))
        if t:
            act(A("hr"), ind(A(h), A("hl")))
        else:
            for s in range(16):
                act(vslot(s), A("vv", c(s, None, 16)))
        ts(A("sI"), spread("M0"), -1.0, O.mult, 1024.0, O.add)
        if t:
            ts(A("i6"), A("i5"), K_("odd"), O.mult, A("Ac", c(1, 2)), O.add)
            ts(A("i1"), A("i5"), A("Ac", c(0, 1)), O.add)
            z = "i1"
        else:
            ts(A("i6"), A("i5"), K_("odd"), O.mult, K_("ev8"), O.add)
            z = "i5"
        ts(A("sI"), A("sI"), 15, O.bitwise_and)
        ts(A("i3"), A("i6"), 3, O.arith_shift_right, 1, O.bitwise_and)
        tt(A("sd"), A("sI"), A("dl"), O.mult)
        group(A("pk", c(480, 488)), [(A("sd"), A("dc128")), (A("Ib"), A("Cl"))])
        tt(A("i4"), A(z), A("i3"), O.mult)
        tt(A("i6"), A("i4"), A("p6", c(0, 128)), O.add)
        ts(A("aI"), A("i6"), 8191, O.bitwise_and)
        for j in range(len(L)):
            tt(blk("hit", j), A("aI"), blk("pn", j), O.is_equal)
        tt(A("nl"), A("p7", c(256, 384)), A("nh"), O.subtract)
        group(A("p5", c(0, 128)), [(A("Ib"), A("ib"))] + [(blk("KZ", s), blk("hit", j)) for j, s in enumerate(L)])
        tt(A("off"), A("aI"), A("p5", c(0, 128)), O.max)
        cp(A("lst"), A("off"))
        tr(A("p6", c(128, 256)), A("off"))
        twin_sums(0)
        if t:
            twin_sums(1)
            twin_flags(0)
            twin_flags(1)

    def reads(t, h):
        win = A("W", c(0, VD))
        A2 = TA // 4 * 2
        act(A("d", c(16 * TA, 2048)), ind(win, A("lst", c(TA, TH))))
        for a, b in ((0, A2), (A2, TA)):
            part = c(16 * a, 16 * b)
            E("v", "tensor_tensor", out=A("d", part), in0=ind(win, A("lst", c(a, b))), in1=A("hr", part), op=O.subtract)
        cp(A("vl"), A("pk", c(480, 488)))
        for a in range(TA, TH, 32):
            b = min(a + 32, TH)
            out = A("pn", c(1024 + 16 * (a - TA), 1024 + 16 * (b - TA)))
            mm(out, A("nI"), A("hr", c(16 * a, 16 * b)), True, False)
            mm(out, A("Ib"), A("d", c(16 * a, 16 * b)), False, True)
        if t == 0:
            twin_sums(1)
        for a, b in ((0, A2), (A2, TA)):
            act(A("ad", c(16 * a, 16 * b)), A("d", c(16 * a, 16 * b)), F.Abs)
        act(A("ad", c(16 * TA, 2048)), A("pn", c(1024, 1024 + 16 * NB)), F.Abs)
        key = A("pk", c(0, 128))
        mm(key, A("Ib"), A("TK"), True, False)
        for k in range(16):
            mm(A("pk", c(k, 128, 16)), A("ad", c(k, None, 16)), A("B16"), False, k == 15)
        if t == 0:
            twin_flags(0)
            twin_flags(1)
        scan(A("sh"), A("r1"), A("d"), O.min, O.max, -128.0)
        scan(A("sl"), A("r2"), A("d"), O.max, O.min, 128.0)
        hi, lo = A("sh", c(15, None, 16)), A("sl", c(15, None, 16))
        scan(A("ME"), A("RS"), key, O.min, O.max, 0.0)
        group(A("p5", c(128, 256)), [(A("nI"), A("x1")), (A("Ib"), A("x2")), (hi, A("B")), (lo, A("nB"))])
        group(A("p5", c(0, 128)), [(hi, A("B")), (lo, A("nB"))])
        mm(A("pn", c(1536, 1664)), A("Ib"), A("mh"), True, False)
        mm(A("pn", c(1536, 1536 + TA)), A("I2"), A(h, c(0, TA)), False, False)
        mm(A("pn", c(1536, 1664)), A("Ib"), hi, False, False)
        mm(A("pn", c(1536, 1664)), A("Ib"), lo, False, True)
        tt(A("oh"), key, A("ME"), O.is_equal)
        if t:
            act(A("no"), A("oh"), scale=-1.0, bias=1.0)
        else:
            tt(A("no"), key, A("ME"), O.not_equal)
        act(A("y1"), A("pn", c(1536, 1664)), scale=0.5, bias=MAGIC)
        act(A("yb"), A("y1"), bias=-MAGIC)
        tt(A("go"), A("p5", c(128, 256)), A("thE"), O.is_ge)
        mm(A("p7", c(0, 128)), A("Ib"), A("ofd"), True, False)
        for k in range(8):
            mm(A("p7", c(16 * k, 16 * k + 16)), blk("eq", k), A("go", c(16 * k, 16 * k + 16)), False, k == 7)
        tt(A("PS"), A("oh"), A("p6", c(128, 256)), O.mult)
        tt(A("Fd"), A("p5", c(0, 128)), A("th2"), O.is_ge)
        scan(A("SE"), A("no"), A("PS"), O.mult, O.add, 0.0)
        tt(A("l2"), A("go"), A("p7", c(0, 128)), O.is_gt)
        ts(A("tg"), spread("SE"), -float(VB), O.add, A("cT", c(t, t + 1)), O.max)
        tt(A("l2"), A("l2"), A("An"), O.mult)
        tt(A("l1"), A("tg"), A("dl"), O.mult)
        group(A("pn", c(1024, 1032)), [(A("I32"), A("Cd")), (A("l2"), A("dc"))])
        act(A("rv", t, rank, c(128, 136)), A("pn", c(1024, 1032)))
        group(A("pn", c(512, 520)), [(A("Fd"), A("rh2")), (A("l1"), A("dc"))])
        cp(A("sl16"), A("pn", c(512, 520)))
        E("v", "tensor_copy", out=ind(A("W", c(VB, WEND)), A("sl16")), in_=A("yb"))
        tt(A("rv", t, rank, c(136, 144)), A("pn", c(1024, 1032)), A("rv", t, rank, c(128, 136)), O.subtract)
        E("v", "tensor_copy", out=A("rv", t, rank, c(0, 128)), in_=ind(A("W", c(VB, VD)), A("vl")))
        toks = []
        need("g", A("rv", t, rank), False, toks)
        settle("g", toks)
        piece = T.rv[:, t, rank, :]
        g.remote_dma_fused([RemoteDMATransfer(dst_ids=[dst(topo, k, core)], dma_engine_mask=bits(es), remote_sem=T.sem["rl%d" % t],
                                              srcs=[piece], dsts=[piece]) for (k, _), es in zip(relay, (loc[:4], e8[:4], loc[4:], e8[4:]))],
                           local_sem=T.sem.lsD)
        g.remote_dma_fused([RemoteDMATransfer(dst_ids=[dst(topo, T.cores[q], core) for q in near], dma_engine_mask=bits(e8),
                                              remote_sem=T.sem["dr%d" % t], srcs=[piece], dsts=[piece for q in near])],
                           local_sem=T.sem.lsD)
        for q in range(NR):
            if q != rank:
                note("rem", A("rv", t, q), True, ("dr%d" % t, len(e8) * (NR - 1), {}))

    def update(t, h, hn):
        group(A("pn", c(0, 128)), [(A("Ib"), A("yb")), (A("nI"), A(h))])
        act(A(hn), A("pn", c(0, 128)), F.Abs)
        group(A("pn", c(1536, 1544)), [(A("yb"), A("B8th")), (A("Ib"), A("c716"))])
        act(A("r8", c(0, 8)), A("pn", c(1536, 1544)), bias=MAGIC)
        act(A("r8", c(8, 16)), A("r8", c(0, 8)), scale=256.0, bias=-256.0 * MAGIC)
        group(A("pn", c(1024, 1032)), [(A("yb"), A("Bm32")), (A("Ib"), A("c960", c(8 * t, 8 * t + 8))), (A("I32"), A("r8", c(8, 16)))])
        if t < STEPS - 1:
            ac = lambda k: A("Ac", c(k, k + 1))
            mm(A("pn", c(512, 640)), A("on32"), A("Fd"), True, True)
            act(A("f1"), A("pn", c(512, 640)), scale=1.0 / 64, bias=-63.0 / 16384, accum_out=ac(2))
            act(ac(3), ac(2), bias=MAGIC)
            act(ac(4), ac(2), scale=64.0, bias=31.5)
            act(ac(5), ac(3), scale=-64.0, bias=64.0 * MAGIC)
            act(ac(0), ac(5), bias=ac(4))
            act(ac(1), ac(0), scale=K_("odd"), bias=K_("ev8"))
        s = lambda k: A("sm", c(8 * k, 8 * k + 8))
        col = lambda n, k: A(n, c(k, 128, 16))
        tt(A("f2"), A("go"), A("e1k"), O.mult)
        ts(s(0), col("SE", 15), float(VB), O.is_lt)
        tt(s(1), col("p5", 15), col("thE", 15), O.is_lt)
        tt(s(3), col("SE", 15), col("nm", t), O.subtract)
        tt(s(2), s(0), s(1), O.mult)
        tt(A("pri"), A("pri"), A("f2"), O.subtract)
        tt(s(3), s(3), s(2), O.mult)
        tt(s(4), A("pn", c(1024, 1032)), s(2), O.mult)
        tt(col("nm", t), col("nm", t), s(3), O.add)
        tt(col("pri", t), col("pri", t), s(4), O.add)

    def drains(t):
        tt(A("dcd"), A("rv", t, c(None), c(128, 136)), A("rv", t, c(None), c(136, 144)), O.add)
        cp(A("dL"), A("dcd"))
        for q in range(NR - 1, -1, -1):
            E("v", "tensor_copy", out=ind(A("W", c(0, VB)), A("dL", c(8 * q, 8 * q + 8))), in_=A("rv", t, q, c(0, 128)))

    fill(A("on32"), 1.0)
    cp(K_("tf"), A("tI"))
    ts(A("thd"), A("I32"), K_("tf"), O.mult)
    mm(A("p5", c(256, 384)), A("on32"), A("thd"), True, True)
    ts(A("xl"), A("mI", c(0, 8)), 16.0, O.mult, 15.0, O.add)
    ts(A("mm"), A("mI"), 15, O.bitwise_and)
    ts(A("dl"), A("mm"), K_("pmf"), O.is_equal)
    ts(A("dc"), A("mI", c(0, 8)), K_("pdf"), O.is_equal)
    ts(A("dc128"), A("dc"), 128.0, O.mult)
    ts(A("Cl"), A("mI", c(0, 8)), 16.0, O.mult, K_("pmf"), O.add)
    ts(K_("nbc"), K_("pf"), -1.0, O.mult, -16384.0 - DUMP, O.add)
    ts(A("tri"), A("dI"), 0, O.is_ge, 16384.0, O.mult)
    for k in range(3):
        ts(A("cT", c(k, k + 1)), K_("pf"), 128.0 * POS[k], O.add)
    ts(A("ofd"), A("mm"), K_("pmf"), O.not_equal, 4.0, O.mult)
    ts(A("B8th"), A("dc"), 0.125, O.mult)
    ts(A("Bm32"), A("dc"), -32.0, O.mult)
    fill(A("c716"), -0.4375)
    for k in range(STEPS):
        fill(A("c960", c(8 * k, 8 * k + 8)), 960.0 - 32 * k)
    ts(A("B16"), A("dc"), 16.0, O.mult)
    ts(A("Cd"), A("Cl"), float(DUMP), O.add)
    ts(A("rh2"), A("dc"), 2048.0, O.mult)
    fill(A("W", c(DUMP, VB)), 0.0)
    fill(A("mh"), -0.5)
    ts(A("th2"), A("ofd"), 1024.0, O.mult)
    act(A("thE"), A("p5", c(256, 384)))
    act(A("nB"), A("B"), scale=-1.0)
    act(A("I2"), A("Ib"), scale=2.0)
    prepare(0, H[0])
    tt(A("th2"), A("thE"), A("th2"), O.add)
    for t in range(STEPS):
        h, hn = H[t % 2], H[1 - t % 2]
        reads(t, h)
        if t == 0:
            for s in (0, 1):
                ts(blk("Sel", s), A("B"), A("oh16", c(s, s + 1)), O.mult)
                act(blk("KZ", s), A("Ib"), scale=float(VB + 128 * (POS[s] + 1)))
        update(t, h, hn)
        if t < STEPS - 1:
            prepare(t + 1, hn)
        else:
            E("y", "dma_start", out=ext("yh"), in_=A(hn))
            for s in range(16):
                act(A("vv", c(s, None, 16)), vslot(s))
            tr(A("pn", c(0, 128)), A("nm"))
            ts(A("sI"), A("pri"), -0.03125, O.mult, 32.0 - 31.0 / 64, O.add)
            ts(A("off"), A("sI"), 31.0, O.min)
            tr(A("pn", c(512, 640)), A("off"))
            cp(A("f1"), A("pn", c(0, 128)))
            cp(A("l1"), A("pn", c(512, 640)))
            E("y", "dma_start", out=ext("ypnd"), in_=A("f1"))
            E("y", "dma_start", out=ext("ydue"), in_=A("l1"))
            E("y", "dma_start", out=ext("yval"), in_=A("vv"))
        drains(t)
    E("y", "dma_start", out=ext("ymem"), in_=A("W", c(rank * C, rank * C + C)))
    g.wait_ge(T.sem.lsD, STEPS * (2 * len(e8) + len(loc)))
    for k in range(ndma[0]):
        if not any(seen[q].get("dm%d" % k, 0) for q in Q):
            g.sync.wait_ge(T.sem["dm%d" % k], 16)
    for q in "gvst":
        if cnt.get("q" + q, 0) > max(seen[o].get("q" + q, 0) for o in Q):
            g.sync.wait_ge(T.sem["q" + q], cnt["q" + q])
